import numpy as np
import ml_dtypes


def mxq(x, axis, fmt="e4m3"):
    dtype, down = {"e4m3": (ml_dtypes.float8_e4m3fn, 7), "e5m2": (ml_dtypes.float8_e5m2, 14)}[fmt]
    v = np.moveaxis(np.asarray(x, np.float32).astype(ml_dtypes.bfloat16).astype(np.float64), axis, -1)
    blocks = v.reshape(v.shape[:-1] + (-1, 32))
    amax = np.abs(blocks).max(-1, keepdims=True)
    byte = np.maximum(np.where(amax > 0, np.frexp(amax)[1] - 1 + 127, 0) - down, 1)
    scale = np.exp2(byte - 127.0)
    codes = (blocks / scale).astype(np.float32).astype(dtype).astype(np.float64)
    return np.moveaxis((codes * scale).reshape(v.shape), -1, axis)


WIDE = False


def mx_kscale(k):
    if not WIDE:
        return np.ones(k)
    levels = np.array([10, -10, 5, -5, 0])
    if k % 512:
        return np.exp2(np.random.permutation(np.resize(levels, k // 32))).repeat(32)
    a = np.empty((k // 512, 16))
    for p in range(k // 512):
        a[p, :8] = np.random.permutation(np.resize(levels, 8))
        for g in range(8):
            far = levels[np.abs(levels - a[p, g]) >= 10]
            a[p, g + 8] = far[np.random.randint(len(far))]
    return np.exp2(a.ravel()).repeat(32)


def f64(x):
    return np.asarray(x).astype(np.float64)


def striped(idx):
    return np.tile(np.asarray(idx).reshape(-1, 16).T, (8, 1)).astype(np.uint16)


def unstriped(offs):
    return offs[:16].T.reshape(-1).astype(np.int64)


B, N, T, D, DV, NQ = 1, 512, 2048, 512, 512, 128


def setup_inputs():
    n = np.random.standard_normal
    idx = np.random.permutation(T)[:B * N]
    s = mx_kscale(D)[:, None]
    u = np.ones(T)
    u[idx] = mx_kscale(B * N)
    r = np.random.uniform(0.5, 2.0, T)
    long = np.random.uniform(0.9, 1.1, T)
    k = n((D, T)) / s * long
    v = n((DV, T)) / (u * r)
    return {
        "qT": (n((B, D, NQ)) * s * (0.90 / np.sqrt(D))).astype(np.float32),
        "kT": k.astype(np.float32),
        "vT": v.astype(np.float32),
        "vs": np.tile(u * r, (128, 1)).astype(np.float32),
        "kb": np.tile(-0.5 * np.sum(np.square(k * s), 0) * (0.90 / np.sqrt(D)), (128, 1)).astype(np.float32),
        "offs": striped(idx),
    }


def reference(qT, kT, vT, vs, kb, offs):
    idx = unstriped(offs)
    k = f64(kT)
    v = f64(vT)
    pick = lambda x: x[:, idx].reshape(x.shape[0], B, N).transpose(1, 0, 2)
    q = f64(qT)
    score = mxq(q, 1, "e4m3").transpose(0, 2, 1) @ mxq(pick(k), 1, "e4m3")
    score = score + pick(f64(kb))[:, :1, :]
    m = score.max(-1, keepdims=True)
    p = np.exp(score - m)
    total = p.sum(-1, keepdims=True)
    w = p * pick(f64(vs))[:, :1, :]
    y = mxq(w, 2, "e4m3") @ mxq(pick(v).transpose(0, 2, 1), 1, "e4m3")
    y = y / total
    return y

@@ -1,0 +1,219 @@
+from contextlib import ExitStack
+
+import concourse.mybir as mybir
+from concourse.masks import make_identity
+
+F32 = mybir.dt.float32
+BF16 = mybir.dt.bfloat16
+U32 = mybir.dt.uint32
+U16 = mybir.dt.uint16
+U8 = mybir.dt.uint8
+FP8X4 = mybir.dt.float8_e4m3fn_x4
+
+P = 128
+POOL = 2048
+SLOTS = 512
+NQ = 128
+D = 512
+DV = 512
+PACK = 4
+PAIRS = 2
+BLOCKS = DV // P
+COLS = SLOTS // P
+
+FLOPS = 2 * NQ * SLOTS * (D + DV)
+BYTES = 4 * ((D + DV) * POOL + 2 * POOL + D * NQ + NQ * DV) + 2 * P * (SLOTS // 16)
+
+
+def tile_attend_rbf_topk_kernel(tc, qT, kT, vT, vs, kb, offs, out):
+    nc = tc.nc
+    exp = mybir.ActivationFunctionType.Exp
+    copy = mybir.ActivationFunctionType.Copy
+    mult, subtract, minimum = mybir.AluOpType.mult, mybir.AluOpType.subtract, mybir.AluOpType.min
+
+    with ExitStack() as ctx:
+        keep = ctx.enter_context(tc.tile_pool(name="keep", bufs=1))
+        over = ctx.enter_context(tc.tile_pool(name="over", bufs=1))
+        psum = ctx.enter_context(tc.psum_pool(name="psum", bufs=2))
+
+        offsets = keep.tile([P, SLOTS // 16], U16, name="offsets")
+        nc.sync.dma_start(offsets[:], offs)
+
+        k_rows = kT.rearrange("(m t) w -> m t w", t=PACK)
+        k_win = [keep.tile([P, POOL], F32, name=f"k_win{t}") for t in range(PACK)]
+        v_win = [keep.tile([P, POOL], F32, name=f"v_win{b}", tag=f"v_win{b}", align_bytes=64) for b in range(BLOCKS - 1)]
+        v_win.append(over.tile([P, POOL], F32, name=f"v_win{BLOCKS - 1}", offset=0, align_bytes=64))
+        q_raw = keep.tile([P, PACK, NQ], F32, name="q_raw")
+        kb_win = keep.tile([P, POOL], F32, name="kb_win")
+        vs_win = keep.tile([P, POOL], F32, name="vs_win")
+        nc.vector.memset(kb_win[:], 0.0)
+        nc.gpsimd.memset(vs_win[:], 0.0)
+        nc.sync.dma_start(k_win[0][:], k_rows[:, 0, :])
+        nc.sync.dma_start(q_raw[:], qT[0].rearrange("(m t) q -> m t q", t=PACK))
+        nc.sync.dma_start(k_win[1][:, 0 : POOL // 2], k_rows[:, 1, 0 : POOL // 2])
+        nc.sync.dma_start(kb_win[0:1, :], kb[0:1, :])
+        nc.sync.dma_start(vs_win[0:1, :], vs[0:1, :])
+        nc.sync.dma_start(k_win[1][:, POOL // 2 :], k_rows[:, 1, POOL // 2 :])
+        for t in range(2, PACK):
+            nc.sync.dma_start(k_win[t][:], k_rows[:, t, :])
+        for b in range(BLOCKS):
+            nc.sync.dma_start(v_win[b][:], vT[b * P : (b + 1) * P, :])
+
+        ident = keep.tile([P, P], F32, name="ident")
+        make_identity(nc, ident[:])
+
+        warm = keep.tile([P, 1], F32, name="warm")
+        nc.scalar.activation(warm[:], ident[:, 0:1], exp)
+
+        v_scales = keep.tile([P, BLOCKS, P], U8, name="v_scales", align_bytes=64)
+        v_sb = [keep.tile([P, SLOTS], BF16, name=f"v_sb{b}") for b in range(BLOCKS)]
+        v_grouped = keep.tile([P, BLOCKS, P, PACK], BF16, name="v_grouped", align_bytes=64)
+        v_codes = {}
+
+        def gather_values(b):
+            nc.vector.tensor_copy(v_sb[b][:].rearrange("p (u m h) -> p m u h", u=PAIRS, h=2), v_win[b][:].indirect(offsets[:]))
+
+        def turn_values(b):
+            words = v_sb[b][:].bitcast(F32)
+            v_turn = psum.tile([P, PAIRS, P], F32, name=f"v_turn{b}", tag="v_turn", bufs=2)
+            for u in range(PAIRS):
+                nc.tensor.transpose(v_turn[:, u, :], words[:, u * P : (u + 1) * P], ident[:])
+            nc.scalar.copy(
+                v_grouped[:, b].rearrange("p e t -> p (e t)").bitcast(F32).rearrange("p (e u) -> p e u", u=PAIRS),
+                v_turn[:].rearrange("p u e -> p e u"),
+            )
+
+        def quantize_values(first, count, codes):
+            nc.vector.quantize_mx(
+                out=codes.bitcast(FP8X4),
+                scales=v_scales[:, first : first + count, :].rearrange("p b e -> p (b e)"),
+                in_=v_grouped[:, first : first + count].rearrange("p b e t -> p (b e t)"),
+            )
+            for b in range(count):
+                v_codes[first + b] = codes[:, b * P : (b + 1) * P]
+
+        k_grouped = keep.tile([P, SLOTS, PACK], BF16, name="k_grouped", align_bytes=64)
+        k_first = keep.tile([P, 2, SLOTS], F32, name="k_first")
+        nc.vector.tensor_copy(k_first[:, 0, :], k_win[0][:].indirect(offsets[:]))
+
+        kb_row = keep.tile([P, SLOTS], F32, name="kb_row")
+        nc.vector.tensor_copy(kb_row[:], kb_win[:].indirect(offsets[:]))
+        vs_row = keep.tile([P, SLOTS], F32, name="vs_row")
+        nc.vector.tensor_copy(vs_row[:], vs_win[:].indirect(offsets[:]))
+
+        q_grouped = keep.tile([P, NQ, PACK], BF16, name="q_grouped", align_bytes=64)
+        q_codes = keep.tile([P, NQ], U32, name="q_codes", align_bytes=64)
+        q_scales = keep.tile([P, NQ], U8, name="q_scales", align_bytes=64)
+        nc.scalar.copy(q_grouped[:], q_raw[:].rearrange("p t q -> p q t"))
+
+        kb_turn = psum.tile([P, COLS, P], F32, name="kb_turn", tag="turn")
+        for c in range(COLS):
+            nc.tensor.transpose(kb_turn[:, c, :], kb_row[:, c * P : (c + 1) * P], ident[:])
+        kb_col = keep.tile([P, COLS], F32, name="kb_col")
+        nc.scalar.copy(kb_col[:], kb_turn[:, :, 0])
+        kb_spread = psum.tile([P, COLS, P], F32, name="kb_spread", tag="turn")
+        for c in range(COLS):
+            nc.tensor.transpose(kb_spread[:, c, :], kb_col[:, c : c + 1].to_broadcast([P, P]), ident[:])
+
+        nc.vector.quantize_mx(out=q_codes[:].bitcast(FP8X4), scales=q_scales[:], in_=q_grouped[:].rearrange("p q t -> p (q t)"))
+
+        nc.vector.tensor_copy(k_first[:, 1, :], k_win[1][:].indirect(offsets[:]))
+        nc.scalar.copy(k_grouped[:, :, 0:2], k_first[:].rearrange("p t i -> p i t"))
+        kb_all = keep.tile([P, SLOTS], F32, name="kb_all")
+        nc.scalar.copy(kb_all[:], kb_spread[:].rearrange("p c i -> p (c i)"))
+
+        vs_perm = keep.tile([P, PACK, P], F32, name="vs_perm")
+        nc.scalar.copy(vs_perm[:].rearrange("p t m -> p m t"), vs_row[:].rearrange("p (m t) -> p m t", t=PACK))
+        vs_turn = psum.tile([P, PACK, P], F32, name="vs_turn", tag="turn")
+        for t in range(PACK):
+            nc.tensor.transpose(vs_turn[:, t, :], vs_perm[:, t, :], ident[:])
+        vs_col = keep.tile([P, PACK], F32, name="vs_col")
+        nc.scalar.copy(vs_col[:], vs_turn[:, :, 0])
+
+        for t in range(2, PACK):
+            nc.vector.tensor_copy(k_grouped[:, :, t], k_win[t][:].indirect(offsets[:]))
+        k_codes = keep.tile([P, SLOTS], U32, name="k_codes", align_bytes=64)
+        k_scales = keep.tile([P, SLOTS], U8, name="k_scales", align_bytes=64)
+        nc.vector.quantize_mx(out=k_codes[:].bitcast(FP8X4), scales=k_scales[:], in_=k_grouped[:].rearrange("p i t -> p (i t)"))
+        score = psum.tile([NQ, SLOTS], F32, name="score", tag="score", bufs=1)
+        nc.tensor.matmul_mx(
+            out=score[:],
+            lhsT=q_codes[:].bitcast(FP8X4),
+            lhsT_scale=q_scales[:],
+            rhs=k_codes[:].bitcast(FP8X4),
+            rhs_scale=k_scales[:],
+            start=True,
+            stop=True,
+        )
+
+        gather_values(0)
+        turn_values(0)
+
+        neg = keep.tile([NQ, SLOTS], F32, name="neg", tag="v_win0", align_bytes=64)
+        nc.vector.scalar_tensor_tensor(neg[:], score[:], -1.0, kb_all[:], mult, subtract)
+        neg_m = keep.tile([NQ, 1], F32, name="neg_m")
+        nc.vector.tensor_reduce(neg_m[:], neg[:], axis=mybir.AxisListType.X, op=minimum)
+        gather_values(1)
+        codes_0 = keep.tile([P, P], U32, name="codes_0", align_bytes=64)
+        quantize_values(0, 1, codes_0[:])
+
+        p = keep.tile([NQ, PACK, P], F32, name="p")
+        total = keep.tile([NQ, 1], F32, name="total")
+        nc.scalar.activation(
+            p[:].rearrange("q t m -> q m t"),
+            neg[:].rearrange("q (m t) -> q m t", t=PACK),
+            exp,
+            bias=neg_m[:],
+            scale=-1.0,
+            accum_out=total[:],
+        )
+        p_turn = psum.tile([P, PACK, NQ], F32, name="p_turn", tag="turn")
+        for t in range(PACK):
+            nc.tensor.transpose(p_turn[:, t, :], p[:, t, :], ident[:])
+        turn_values(1)
+        gather_values(2)
+        gather_values(3)
+
+        w_grouped = over.tile([P, NQ, PACK], BF16, name="w_grouped", offset=0, align_bytes=64)
+        nc.vector.tensor_tensor(
+            w_grouped[:],
+            p_turn[:].rearrange("m t q -> m q t"),
+            vs_col[:].unsqueeze(1).to_broadcast([P, NQ, PACK]),
+            mult,
+        )
+        turn_values(2)
+        codes_12 = over.tile([P, 2 * P], U32, name="codes_12", offset=2 * NQ * PACK, align_bytes=64)
+        quantize_values(1, 2, codes_12[:])
+        w_codes = keep.tile([P, NQ], U32, name="w_codes", align_bytes=64)
+        w_scales = keep.tile([P, NQ], U8, name="w_scales", align_bytes=64)
+        nc.vector.quantize_mx(out=w_codes[:].bitcast(FP8X4), scales=w_scales[:], in_=w_grouped[:].rearrange("p q t -> p (q t)"))
+        inverse = keep.tile([NQ, 1], F32, name="inverse")
+        nc.vector.reciprocal(inverse[:], total[:])
+        turn_values(3)
+        codes_3 = keep.tile([P, P], U32, name="codes_3", align_bytes=64)
+        quantize_values(3, 1, codes_3[:])
+
+        def product(y, b):
+            nc.tensor.matmul_mx(
+                out=y,
+                lhsT=w_codes[:].bitcast(FP8X4),
+                lhsT_scale=w_scales[:],
+                rhs=v_codes[b].bitcast(FP8X4),
+                rhs_scale=v_scales[:, b, :],
+                start=True,
+                stop=True,
+            )
+
+        y_first = psum.tile([NQ, 2, P], F32, name="y_first", tag="y")
+        y_last = psum.tile([NQ, 2, P], F32, name="y_last", tag="y")
+        for b in range(2):
+            product(y_first[:, b, :], b)
+        out_first = keep.tile([NQ, 2 * P], F32, name="out_first")
+        nc.scalar.activation(out_first[:], y_first[:].rearrange("q b e -> q (b e)"), copy, scale=inverse[:])
+        nc.scalar.dma_start(out[0, :, 0 : 2 * P], out_first[:])
+
+        for b in range(2):
+            product(y_last[:, b, :], 2 + b)
+        out_last = keep.tile([NQ, 2 * P], F32, name="out_last")
+        nc.vector.tensor_scalar(out_last[:], y_last[:].rearrange("q b e -> q (b e)"), inverse[:], None, mult)
+        nc.sync.dma_start(out[0, :, 2 * P : DV], out_last[:])

@@ -19,6 +19,8 @@ DV = 512
 PACK = 4
 PAIRS = 2
 BLOCKS = DV // P
+KB_ROW = P - 1
+VS_ROW = P // 2 - 1
 COLS = SLOTS // P
 
 FLOPS = 2 * NQ * SLOTS * (D + DV)
@@ -37,7 +39,6 @@ def tile_attend_rbf_topk_kernel(tc, qT, kT, vT, vs, kb, offs, out):
         psum = ctx.enter_context(tc.psum_pool(name="psum", bufs=2))
 
         offsets = keep.tile([P, SLOTS // 16], U16, name="offsets")
-        nc.sync.dma_start(offsets[:], offs)
 
         k_rows = kT.rearrange("(m t) w -> m t w", t=PACK)
         k_win = [keep.tile([P, POOL], F32, name=f"k_win{t}") for t in range(PACK)]
@@ -46,21 +47,21 @@ def tile_attend_rbf_topk_kernel(tc, qT, kT, vT, vs, kb, offs, out):
         q_raw = keep.tile([P, PACK, NQ], F32, name="q_raw")
         kb_win = keep.tile([P, POOL], F32, name="kb_win")
         vs_win = keep.tile([P, POOL], F32, name="vs_win")
-        nc.vector.memset(kb_win[:], 0.0)
-        nc.gpsimd.memset(vs_win[:], 0.0)
         nc.sync.dma_start(k_win[0][:], k_rows[:, 0, :])
+        nc.sync.dma_start(offsets[:], offs)
+        nc.sync.dma_start(kb_win[KB_ROW : KB_ROW + 1, :], kb[0:1, :])
+        nc.sync.dma_start(vs_win[VS_ROW : VS_ROW + 1, :], vs[0:1, :])
         nc.sync.dma_start(q_raw[:], qT[0].rearrange("(m t) q -> m t q", t=PACK))
-        nc.sync.dma_start(k_win[1][:, 0 : POOL // 2], k_rows[:, 1, 0 : POOL // 2])
-        nc.sync.dma_start(kb_win[0:1, :], kb[0:1, :])
-        nc.sync.dma_start(vs_win[0:1, :], vs[0:1, :])
-        nc.sync.dma_start(k_win[1][:, POOL // 2 :], k_rows[:, 1, POOL // 2 :])
-        for t in range(2, PACK):
+        for t in range(1, PACK):
             nc.sync.dma_start(k_win[t][:], k_rows[:, t, :])
         for b in range(BLOCKS):
             nc.sync.dma_start(v_win[b][:], vT[b * P : (b + 1) * P, :])
 
         ident = keep.tile([P, P], F32, name="ident")
         make_identity(nc, ident[:])
+        nc.vector.memset(kb_win[0:KB_ROW, :], 0.0)
+        nc.vector.memset(vs_win[0:VS_ROW, :], 0.0)
+        nc.gpsimd.memset(vs_win[VS_ROW + 1 : P, :], 0.0)
 
         warm = keep.tile([P, 1], F32, name="warm")
         nc.scalar.activation(warm[:], ident[:, 0:1], exp)
@@ -110,7 +111,7 @@ def tile_attend_rbf_topk_kernel(tc, qT, kT, vT, vs, kb, offs, out):
         for c in range(COLS):
             nc.tensor.transpose(kb_turn[:, c, :], kb_row[:, c * P : (c + 1) * P], ident[:])
         kb_col = keep.tile([P, COLS], F32, name="kb_col")
-        nc.scalar.copy(kb_col[:], kb_turn[:, :, 0])
+        nc.scalar.copy(kb_col[:], kb_turn[:, :, KB_ROW])
         kb_spread = psum.tile([P, COLS, P], F32, name="kb_spread", tag="turn")
         for c in range(COLS):
             nc.tensor.transpose(kb_spread[:, c, :], kb_col[:, c : c + 1].to_broadcast([P, P]), ident[:])
@@ -128,7 +129,7 @@ def tile_attend_rbf_topk_kernel(tc, qT, kT, vT, vs, kb, offs, out):
         for t in range(PACK):
             nc.tensor.transpose(vs_turn[:, t, :], vs_perm[:, t, :], ident[:])
         vs_col = keep.tile([P, PACK], F32, name="vs_col")
-        nc.scalar.copy(vs_col[:], vs_turn[:, :, 0])
+        nc.scalar.copy(vs_col[:], vs_turn[:, :, VS_ROW])
 
         for t in range(2, PACK):
             nc.vector.tensor_copy(k_grouped[:, :, t], k_win[t][:].indirect(offsets[:]))

@@ -172,20 +172,16 @@ def tile_attend_rbf_topk_kernel(tc, qT, kT, vT, vs, kb, offs, out):
         for t in range(PACK):
             nc.tensor.transpose(p_turn[:, t, :], p[:, t, :], ident[:])
         turn_values(1)
+
+        w_grouped = keep.tile([P, NQ, PACK], BF16, name="w_grouped", align_bytes=64)
+        for t in range(PACK):
+            nc.scalar.activation(w_grouped[:, :, t], p_turn[:, t, :], copy, scale=vs_col[:, t : t + 1])
         gather_values(2)
         gather_values(3)
-
-        w_grouped = over.tile([P, NQ, PACK], BF16, name="w_grouped", offset=0, align_bytes=64)
-        nc.vector.tensor_tensor(
-            w_grouped[:],
-            p_turn[:].rearrange("m t q -> m q t"),
-            vs_col[:].unsqueeze(1).to_broadcast([P, NQ, PACK]),
-            mult,
-        )
         turn_values(2)
-        codes_12 = over.tile([P, 2 * P], U32, name="codes_12", offset=2 * NQ * PACK, align_bytes=64)
+        codes_12 = over.tile([P, 2 * P], U32, name="codes_12", offset=0, align_bytes=64)
+        w_codes = over.tile([P, NQ], U32, name="w_codes", offset=4 * 2 * P, align_bytes=64)
         quantize_values(1, 2, codes_12[:])
-        w_codes = keep.tile([P, NQ], U32, name="w_codes", align_bytes=64)
         w_scales = keep.tile([P, NQ], U8, name="w_scales", align_bytes=64)
         nc.vector.quantize_mx(out=w_codes[:].bitcast(FP8X4), scales=w_scales[:], in_=w_grouped[:].rearrange("p q t -> p (q t)"))
         inverse = keep.tile([NQ, 1], F32, name="inverse")

@@ -202,15 +202,20 @@ def tile_attend_rbf_topk_kernel(tc, qT, kT, vT, vs, kb, offs, out):
             )
 
         y_first = psum.tile([NQ, 2, P], F32, name="y_first", tag="y")
-        y_last = psum.tile([NQ, 2, P], F32, name="y_last", tag="y")
         for b in range(2):
             product(y_first[:, b, :], b)
         out_first = keep.tile([NQ, 2 * P], F32, name="out_first")
         nc.scalar.activation(out_first[:], y_first[:].rearrange("q b e -> q (b e)"), copy, scale=inverse[:])
         nc.scalar.dma_start(out[0, :, 0 : 2 * P], out_first[:])
 
-        for b in range(2):
-            product(y_last[:, b, :], 2 + b)
-        out_last = keep.tile([NQ, 2 * P], F32, name="out_last")
-        nc.vector.tensor_scalar(out_last[:], y_last[:].rearrange("q b e -> q (b e)"), inverse[:], None, mult)
-        nc.sync.dma_start(out[0, :, 2 * P : DV], out_last[:])
+        y_next = psum.tile([NQ, P], F32, name="y_next", tag="y")
+        product(y_next[:], 2)
+        out_next = keep.tile([NQ, P], F32, name="out_next")
+        nc.scalar.activation(out_next[:], y_next[:], copy, scale=inverse[:])
+        nc.scalar.dma_start(out[0, :, 2 * P : 3 * P], out_next[:])
+
+        y_last = psum.tile([NQ, P], F32, name="y_last", tag="score", bufs=1)
+        product(y_last[:], 3)
+        out_last = keep.tile([NQ, P], F32, name="out_last")
+        nc.vector.tensor_scalar(out_last[:], y_last[:], inverse[:], None, mult)
+        nc.sync.dma_start(out[0, :, 3 * P : DV], out_last[:])

@@ -21,6 +21,8 @@ PAIRS = 2
 BLOCKS = DV // P
 KB_ROW = P - 1
 VS_ROW = P // 2 - 1
+WINDOW_BYTES = 4 * POOL
+HALF = SLOTS // 2
 COLS = SLOTS // P
 
 FLOPS = 2 * NQ * SLOTS * (D + DV)
@@ -42,8 +44,7 @@ def tile_attend_rbf_topk_kernel(tc, qT, kT, vT, vs, kb, offs, out):
 
         k_rows = kT.rearrange("(m t) w -> m t w", t=PACK)
         k_win = [keep.tile([P, POOL], F32, name=f"k_win{t}") for t in range(PACK)]
-        v_win = [keep.tile([P, POOL], F32, name=f"v_win{b}", tag=f"v_win{b}", align_bytes=64) for b in range(BLOCKS - 1)]
-        v_win.append(over.tile([P, POOL], F32, name=f"v_win{BLOCKS - 1}", offset=0, align_bytes=64))
+        v_win = [over.tile([P, POOL], F32, name=f"v_win{b}", offset=b * WINDOW_BYTES, align_bytes=64) for b in range(BLOCKS)]
         q_raw = keep.tile([P, PACK, NQ], F32, name="q_raw")
         kb_win = keep.tile([P, POOL], F32, name="kb_win")
         vs_win = keep.tile([P, POOL], F32, name="vs_win")
@@ -131,32 +132,35 @@ def tile_attend_rbf_topk_kernel(tc, qT, kT, vT, vs, kb, offs, out):
         vs_col = keep.tile([P, PACK], F32, name="vs_col")
         nc.scalar.copy(vs_col[:], vs_turn[:, :, VS_ROW])
 
-        for t in range(2, PACK):
-            nc.vector.tensor_copy(k_grouped[:, :, t], k_win[t][:].indirect(offsets[:]))
+        nc.vector.tensor_copy(k_grouped[:, :, 2], k_win[2][:].indirect(offsets[:]))
+        halves = [slice(h * HALF, (h + 1) * HALF) for h in range(2)]
+        for h in range(2):
+            listed = offsets[:, h * (HALF // 16) : (h + 1) * (HALF // 16)]
+            nc.vector.tensor_copy(k_grouped[:, halves[h], 3], k_win[3][:].indirect(listed))
         k_codes = keep.tile([P, SLOTS], U32, name="k_codes", align_bytes=64)
         k_scales = keep.tile([P, SLOTS], U8, name="k_scales", align_bytes=64)
-        nc.vector.quantize_mx(out=k_codes[:].bitcast(FP8X4), scales=k_scales[:], in_=k_grouped[:].rearrange("p i t -> p (i t)"))
-        score = psum.tile([NQ, SLOTS], F32, name="score", tag="score", bufs=1)
-        nc.tensor.matmul_mx(
-            out=score[:],
-            lhsT=q_codes[:].bitcast(FP8X4),
-            lhsT_scale=q_scales[:],
-            rhs=k_codes[:].bitcast(FP8X4),
-            rhs_scale=k_scales[:],
-            start=True,
-            stop=True,
-        )
+        score = [psum.tile([NQ, HALF], F32, name=f"score{h}", tag="score", bufs=2) for h in range(2)]
+        for h in range(2):
+            nc.vector.quantize_mx(
+                out=k_codes[:, halves[h]].bitcast(FP8X4),
+                scales=k_scales[:, halves[h]],
+                in_=k_grouped[:, halves[h], :].rearrange("p i t -> p (i t)"),
+            )
+            nc.tensor.matmul_mx(
+                out=score[h][:],
+                lhsT=q_codes[:].bitcast(FP8X4),
+                lhsT_scale=q_scales[:],
+                rhs=k_codes[:, halves[h]].bitcast(FP8X4),
+                rhs_scale=k_scales[:, halves[h]],
+                start=True,
+                stop=True,
+            )
 
-        gather_values(0)
-        turn_values(0)
-
-        neg = keep.tile([NQ, SLOTS], F32, name="neg", tag="v_win0", align_bytes=64)
-        nc.vector.scalar_tensor_tensor(neg[:], score[:], -1.0, kb_all[:], mult, subtract)
+        neg = keep.tile([NQ, SLOTS], F32, name="neg")
+        for h in range(2):
+            nc.vector.scalar_tensor_tensor(neg[:, halves[h]], score[h][:], -1.0, kb_all[:, halves[h]], mult, subtract)
         neg_m = keep.tile([NQ, 1], F32, name="neg_m")
         nc.vector.tensor_reduce(neg_m[:], neg[:], axis=mybir.AxisListType.X, op=minimum)
-        gather_values(1)
-        codes_0 = keep.tile([P, P], U32, name="codes_0", align_bytes=64)
-        quantize_values(0, 1, codes_0[:])
 
         p = keep.tile([NQ, PACK, P], F32, name="p")
         total = keep.tile([NQ, 1], F32, name="total")
@@ -171,21 +175,23 @@ def tile_attend_rbf_topk_kernel(tc, qT, kT, vT, vs, kb, offs, out):
         p_turn = psum.tile([P, PACK, NQ], F32, name="p_turn", tag="turn")
         for t in range(PACK):
             nc.tensor.transpose(p_turn[:, t, :], p[:, t, :], ident[:])
-        turn_values(1)
 
         w_grouped = keep.tile([P, NQ, PACK], BF16, name="w_grouped", align_bytes=64)
         for t in range(PACK):
             nc.scalar.activation(w_grouped[:, :, t], p_turn[:, t, :], copy, scale=vs_col[:, t : t + 1])
-        gather_values(2)
+        for b in range(BLOCKS - 1):
+            gather_values(b)
+            turn_values(b)
+        codes_0 = over.tile([P, P], U32, name="codes_0", offset=2 * WINDOW_BYTES, align_bytes=64)
+        inverse = over.tile([NQ, 1], F32, name="inverse", offset=2 * WINDOW_BYTES + 4 * P, align_bytes=64)
+        quantize_values(0, 1, codes_0[:])
+        nc.vector.reciprocal(inverse[:], total[:])
         gather_values(3)
-        turn_values(2)
-        codes_12 = over.tile([P, 2 * P], U32, name="codes_12", offset=0, align_bytes=64)
-        w_codes = over.tile([P, NQ], U32, name="w_codes", offset=4 * 2 * P, align_bytes=64)
+        codes_12 = over.tile([P, 2 * P], U32, name="codes_12", offset=3 * WINDOW_BYTES, align_bytes=64)
+        w_codes = over.tile([P, NQ], U32, name="w_codes", offset=3 * WINDOW_BYTES + 4 * 2 * P, align_bytes=64)
         quantize_values(1, 2, codes_12[:])
         w_scales = keep.tile([P, NQ], U8, name="w_scales", align_bytes=64)
         nc.vector.quantize_mx(out=w_codes[:].bitcast(FP8X4), scales=w_scales[:], in_=w_grouped[:].rearrange("p q t -> p (q t)"))
-        inverse = keep.tile([NQ, 1], F32, name="inverse")
-        nc.vector.reciprocal(inverse[:], total[:])
         turn_values(3)
         codes_3 = keep.tile([P, P], U32, name="codes_3", align_bytes=64)
         quantize_values(3, 1, codes_3[:])
@@ -214,7 +220,7 @@ def tile_attend_rbf_topk_kernel(tc, qT, kT, vT, vs, kb, offs, out):
         nc.scalar.activation(out_next[:], y_next[:], copy, scale=inverse[:])
         nc.scalar.dma_start(out[0, :, 2 * P : 3 * P], out_next[:])
 
-        y_last = psum.tile([NQ, P], F32, name="y_last", tag="score", bufs=1)
+        y_last = psum.tile([NQ, P], F32, name="y_last", tag="score", bufs=2)
         product(y_last[:], 3)
         out_last = keep.tile([NQ, P], F32, name="out_last")
         nc.vector.tensor_scalar(out_last[:], y_last[:], inverse[:], None, mult)

@@ -75,15 +75,17 @@ def tile_attend_rbf_topk_kernel(tc, qT, kT, vT, vs, kb, offs, out):
         def gather_values(b):
             nc.vector.tensor_copy(v_sb[b][:].rearrange("p (u m h) -> p m u h", u=PAIRS, h=2), v_win[b][:].indirect(offsets[:]))
 
-        def turn_values(b):
+        def turn_values(b, pieces=1):
             words = v_sb[b][:].bitcast(F32)
             v_turn = psum.tile([P, PAIRS, P], F32, name=f"v_turn{b}", tag="v_turn", bufs=2)
             for u in range(PAIRS):
                 nc.tensor.transpose(v_turn[:, u, :], words[:, u * P : (u + 1) * P], ident[:])
-            nc.scalar.copy(
-                v_grouped[:, b].rearrange("p e t -> p (e t)").bitcast(F32).rearrange("p (e u) -> p e u", u=PAIRS),
-                v_turn[:].rearrange("p u e -> p e u"),
-            )
+            for j in range(pieces):
+                part = slice(j * P // pieces, (j + 1) * P // pieces)
+                nc.scalar.copy(
+                    v_grouped[:, b, part].rearrange("p e t -> p (e t)").bitcast(F32).rearrange("p (e u) -> p e u", u=PAIRS),
+                    v_turn[:, :, part].rearrange("p u e -> p e u"),
+                )
 
         def quantize_values(first, count, codes):
             nc.vector.quantize_mx(
@@ -182,19 +184,25 @@ def tile_attend_rbf_topk_kernel(tc, qT, kT, vT, vs, kb, offs, out):
         for b in range(BLOCKS - 1):
             gather_values(b)
             turn_values(b)
-        codes_0 = over.tile([P, P], U32, name="codes_0", offset=2 * WINDOW_BYTES, align_bytes=64)
-        inverse = over.tile([NQ, 1], F32, name="inverse", offset=2 * WINDOW_BYTES + 4 * P, align_bytes=64)
-        quantize_values(0, 1, codes_0[:])
+        inverse = over.tile([NQ, 1], F32, name="inverse", offset=2 * WINDOW_BYTES, align_bytes=64)
         nc.vector.reciprocal(inverse[:], total[:])
         gather_values(3)
-        codes_12 = over.tile([P, 2 * P], U32, name="codes_12", offset=3 * WINDOW_BYTES, align_bytes=64)
+        codes_01 = over.tile([P, 2 * P], U32, name="codes_01", offset=3 * WINDOW_BYTES, align_bytes=64)
+        codes_2 = over.tile([P, P], U32, name="codes_2", offset=3 * WINDOW_BYTES + 4 * 3 * P, align_bytes=64)
         w_codes = over.tile([P, NQ], U32, name="w_codes", offset=3 * WINDOW_BYTES + 4 * 2 * P, align_bytes=64)
-        quantize_values(1, 2, codes_12[:])
+        quantize_values(0, 2, codes_01[:])
         w_scales = keep.tile([P, NQ], U8, name="w_scales", align_bytes=64)
         nc.vector.quantize_mx(out=w_codes[:].bitcast(FP8X4), scales=w_scales[:], in_=w_grouped[:].rearrange("p q t -> p (q t)"))
-        turn_values(3)
+        quantize_values(2, 1, codes_2[:])
+        turn_values(3, pieces=2)
         codes_3 = keep.tile([P, P], U32, name="codes_3", align_bytes=64)
-        quantize_values(3, 1, codes_3[:])
+        parts = [slice(j * P // 2, (j + 1) * P // 2) for j in range(2)]
+        for part in parts:
+            nc.vector.quantize_mx(
+                out=codes_3[:, part].bitcast(FP8X4),
+                scales=v_scales[:, 3, part],
+                in_=v_grouped[:, 3, part].rearrange("p e t -> p (e t)"),
+            )
 
         def product(y, b):
             nc.tensor.matmul_mx(
@@ -212,16 +220,25 @@ def tile_attend_rbf_topk_kernel(tc, qT, kT, vT, vs, kb, offs, out):
             product(y_first[:, b, :], b)
         out_first = keep.tile([NQ, 2 * P], F32, name="out_first")
         nc.scalar.activation(out_first[:], y_first[:].rearrange("q b e -> q (b e)"), copy, scale=inverse[:])
-        nc.scalar.dma_start(out[0, :, 0 : 2 * P], out_first[:])
+        nc.sync.dma_start(out[0, :, 0 : 2 * P], out_first[:])
 
         y_next = psum.tile([NQ, P], F32, name="y_next", tag="y")
         product(y_next[:], 2)
         out_next = keep.tile([NQ, P], F32, name="out_next")
         nc.scalar.activation(out_next[:], y_next[:], copy, scale=inverse[:])
-        nc.scalar.dma_start(out[0, :, 2 * P : 3 * P], out_next[:])
+        nc.sync.dma_start(out[0, :, 2 * P : 3 * P], out_next[:])
 
-        y_last = psum.tile([NQ, P], F32, name="y_last", tag="score", bufs=2)
-        product(y_last[:], 3)
         out_last = keep.tile([NQ, P], F32, name="out_last")
-        nc.vector.tensor_scalar(out_last[:], y_last[:], inverse[:], None, mult)
+        y_last = [psum.tile([NQ, P // 2], F32, name=f"y_last{j}", tag="score", bufs=2) for j in range(2)]
+        for j, part in enumerate(parts):
+            nc.tensor.matmul_mx(
+                out=y_last[j][:],
+                lhsT=w_codes[:].bitcast(FP8X4),
+                lhsT_scale=w_scales[:],
+                rhs=codes_3[:, part].bitcast(FP8X4),
+                rhs_scale=v_scales[:, 3, part],
+                start=True,
+                stop=True,
+            )
+            nc.vector.tensor_scalar(out_last[:, part], y_last[j][:], inverse[:], None, mult)
         nc.sync.dma_start(out[0, :, 3 * P : DV], out_last[:])

@@ -126,13 +126,16 @@ def tile_attend_rbf_topk_kernel(tc, qT, kT, vT, vs, kb, offs, out):
         kb_all = keep.tile([P, SLOTS], F32, name="kb_all")
         nc.scalar.copy(kb_all[:], kb_spread[:].rearrange("p c i -> p (c i)"))
 
-        vs_perm = keep.tile([P, PACK, P], F32, name="vs_perm")
-        nc.scalar.copy(vs_perm[:].rearrange("p t m -> p m t"), vs_row[:].rearrange("p (m t) -> p m t", t=PACK))
-        vs_turn = psum.tile([P, PACK, P], F32, name="vs_turn", tag="turn")
-        for t in range(PACK):
-            nc.tensor.transpose(vs_turn[:, t, :], vs_perm[:, t, :], ident[:])
-        vs_col = keep.tile([P, PACK], F32, name="vs_col")
+        vs_turn = psum.tile([P, COLS, P], F32, name="vs_turn", tag="turn")
+        for c in range(COLS):
+            nc.tensor.transpose(vs_turn[:, c, :], vs_row[:, c * P : (c + 1) * P], ident[:])
+        vs_col = keep.tile([P, COLS], F32, name="vs_col")
         nc.scalar.copy(vs_col[:], vs_turn[:, :, VS_ROW])
+        vs_spread = psum.tile([P, COLS, P], F32, name="vs_spread", tag="turn")
+        for c in range(COLS):
+            nc.tensor.transpose(vs_spread[:, c, :], vs_col[:, c : c + 1].to_broadcast([P, P]), ident[:])
+        vs_all = keep.tile([P, SLOTS], F32, name="vs_all")
+        nc.scalar.copy(vs_all[:], vs_spread[:].rearrange("p c i -> p (c i)"))
 
         nc.vector.tensor_copy(k_grouped[:, :, 2], k_win[2][:].indirect(offsets[:]))
         halves = [slice(h * HALF, (h + 1) * HALF) for h in range(2)]
@@ -164,32 +167,29 @@ def tile_attend_rbf_topk_kernel(tc, qT, kT, vT, vs, kb, offs, out):
         neg_m = keep.tile([NQ, 1], F32, name="neg_m")
         nc.vector.tensor_reduce(neg_m[:], neg[:], axis=mybir.AxisListType.X, op=minimum)
 
-        p = keep.tile([NQ, PACK, P], F32, name="p")
+        p = keep.tile([NQ, SLOTS], F32, name="p")
         total = keep.tile([NQ, 1], F32, name="total")
-        nc.scalar.activation(
-            p[:].rearrange("q t m -> q m t"),
-            neg[:].rearrange("q (m t) -> q m t", t=PACK),
-            exp,
-            bias=neg_m[:],
-            scale=-1.0,
-            accum_out=total[:],
-        )
-        p_turn = psum.tile([P, PACK, NQ], F32, name="p_turn", tag="turn")
-        for t in range(PACK):
-            nc.tensor.transpose(p_turn[:, t, :], p[:, t, :], ident[:])
+        nc.scalar.activation(p[:], neg[:], exp, bias=neg_m[:], scale=-1.0, accum_out=total[:])
 
+        w_sb = keep.tile([NQ, SLOTS], BF16, name="w_sb")
+        nc.gpsimd.tensor_tensor(w_sb[:], p[:], vs_all[:], mult)
+        w_turn = psum.tile([P, PAIRS, NQ], F32, name="w_turn", tag="turn")
+        for u in range(PAIRS):
+            nc.tensor.transpose(w_turn[:, u, :], w_sb[:].bitcast(F32)[:, u : PAIRS * P : PAIRS], ident[:])
         w_grouped = keep.tile([P, NQ, PACK], BF16, name="w_grouped", align_bytes=64)
-        for t in range(PACK):
-            nc.scalar.activation(w_grouped[:, :, t], p_turn[:, t, :], copy, scale=vs_col[:, t : t + 1])
+        nc.scalar.copy(
+            w_grouped[:].rearrange("p q t -> p (q t)").bitcast(F32).rearrange("p (q u) -> p q u", u=PAIRS),
+            w_turn[:].rearrange("p u q -> p q u"),
+        )
         for b in range(BLOCKS - 1):
             gather_values(b)
             turn_values(b)
         inverse = over.tile([NQ, 1], F32, name="inverse", offset=2 * WINDOW_BYTES, align_bytes=64)
         nc.vector.reciprocal(inverse[:], total[:])
         gather_values(3)
-        codes_01 = over.tile([P, 2 * P], U32, name="codes_01", offset=3 * WINDOW_BYTES, align_bytes=64)
+        codes_01 = over.tile([P, 2 * P], U32, name="codes_01", offset=2 * WINDOW_BYTES + 4 * 2 * P, align_bytes=64)
         codes_2 = over.tile([P, P], U32, name="codes_2", offset=3 * WINDOW_BYTES + 4 * 3 * P, align_bytes=64)
-        w_codes = over.tile([P, NQ], U32, name="w_codes", offset=3 * WINDOW_BYTES + 4 * 2 * P, align_bytes=64)
+        w_codes = over.tile([P, NQ], U32, name="w_codes", offset=2 * WINDOW_BYTES + 4 * P, align_bytes=64)
         quantize_values(0, 2, codes_01[:])
         w_scales = keep.tile([P, NQ], U8, name="w_scales", align_bytes=64)
         nc.vector.quantize_mx(out=w_codes[:].bitcast(FP8X4), scales=w_scales[:], in_=w_grouped[:].rearrange("p q t -> p (q t)"))

@@ -187,9 +187,9 @@ def tile_attend_rbf_topk_kernel(tc, qT, kT, vT, vs, kb, offs, out):
         inverse = over.tile([NQ, 1], F32, name="inverse", offset=2 * WINDOW_BYTES, align_bytes=64)
         nc.vector.reciprocal(inverse[:], total[:])
         gather_values(3)
-        codes_01 = over.tile([P, 2 * P], U32, name="codes_01", offset=2 * WINDOW_BYTES + 4 * 2 * P, align_bytes=64)
+        codes_01 = over.tile([P, 2 * P], U32, name="codes_01", offset=3 * WINDOW_BYTES, align_bytes=64)
         codes_2 = over.tile([P, P], U32, name="codes_2", offset=3 * WINDOW_BYTES + 4 * 3 * P, align_bytes=64)
-        w_codes = over.tile([P, NQ], U32, name="w_codes", offset=2 * WINDOW_BYTES + 4 * P, align_bytes=64)
+        w_codes = over.tile([P, NQ], U32, name="w_codes", offset=3 * WINDOW_BYTES + 4 * 2 * P, align_bytes=64)
         quantize_values(0, 2, codes_01[:])
         w_scales = keep.tile([P, NQ], U8, name="w_scales", align_bytes=64)
         nc.vector.quantize_mx(out=w_codes[:].bitcast(FP8X4), scales=w_scales[:], in_=w_grouped[:].rearrange("p q t -> p (q t)"))

@@ -50,9 +50,9 @@ def tile_attend_rbf_topk_kernel(tc, qT, kT, vT, vs, kb, offs, out):
         vs_win = keep.tile([P, POOL], F32, name="vs_win")
         nc.sync.dma_start(k_win[0][:], k_rows[:, 0, :])
         nc.sync.dma_start(offsets[:], offs)
-        nc.sync.dma_start(kb_win[KB_ROW : KB_ROW + 1, :], kb[0:1, :])
-        nc.sync.dma_start(vs_win[VS_ROW : VS_ROW + 1, :], vs[0:1, :])
-        nc.sync.dma_start(q_raw[:], qT[0].rearrange("(m t) q -> m t q", t=PACK))
+        nc.scalar.dma_start(kb_win[KB_ROW : KB_ROW + 1, :], kb[0:1, :])
+        nc.scalar.dma_start(vs_win[VS_ROW : VS_ROW + 1, :], vs[0:1, :])
+        nc.scalar.dma_start(q_raw[:], qT[0].rearrange("(m t) q -> m t q", t=PACK))
         for t in range(1, PACK):
             nc.sync.dma_start(k_win[t][:], k_rows[:, t, :])
         for b in range(BLOCKS):

@@ -43,20 +43,25 @@ def tile_attend_rbf_topk_kernel(tc, qT, kT, vT, vs, kb, offs, out):
         offsets = keep.tile([P, SLOTS // 16], U16, name="offsets")
 
         k_rows = kT.rearrange("(m t) w -> m t w", t=PACK)
-        k_win = [keep.tile([P, POOL], F32, name=f"k_win{t}") for t in range(PACK)]
-        v_win = [over.tile([P, POOL], F32, name=f"v_win{b}", offset=b * WINDOW_BYTES, align_bytes=64) for b in range(BLOCKS)]
+        k_pair = keep.tile([P, 2, POOL], F32, name="k_pair")
+        k_rest = [keep.tile([P, POOL], F32, name=f"k_win{t}") for t in range(2, PACK)]
+        k_win = [k_pair[:, 0, :], k_pair[:, 1, :], k_rest[0][:], k_rest[1][:]]
+        v_pair = over.tile([P, 2, POOL], F32, name="v_pair", offset=0, align_bytes=64)
+        v_rest = [over.tile([P, POOL], F32, name=f"v_win{b}", offset=b * WINDOW_BYTES, align_bytes=64) for b in range(2, BLOCKS)]
+        v_win = [v_pair[:, 0, :], v_pair[:, 1, :], v_rest[0][:], v_rest[1][:]]
         q_raw = keep.tile([P, PACK, NQ], F32, name="q_raw")
         kb_win = keep.tile([P, POOL], F32, name="kb_win")
         vs_win = keep.tile([P, POOL], F32, name="vs_win")
-        nc.sync.dma_start(k_win[0][:], k_rows[:, 0, :])
+        nc.sync.dma_start(q_raw[:], qT[0].rearrange("(m t) q -> m t q", t=PACK))
         nc.sync.dma_start(offsets[:], offs)
-        nc.scalar.dma_start(kb_win[KB_ROW : KB_ROW + 1, :], kb[0:1, :])
-        nc.scalar.dma_start(vs_win[VS_ROW : VS_ROW + 1, :], vs[0:1, :])
-        nc.scalar.dma_start(q_raw[:], qT[0].rearrange("(m t) q -> m t q", t=PACK))
-        for t in range(1, PACK):
-            nc.sync.dma_start(k_win[t][:], k_rows[:, t, :])
-        for b in range(BLOCKS):
-            nc.sync.dma_start(v_win[b][:], vT[b * P : (b + 1) * P, :])
+        nc.sync.dma_start(kb_win[KB_ROW : KB_ROW + 1, :], kb[0:1, :])
+        nc.sync.dma_start(vs_win[VS_ROW : VS_ROW + 1, :], vs[0:1, :])
+        nc.sync.dma_start(k_pair[:], k_rows[:, 0:2, :])
+        for t in range(2, PACK):
+            nc.sync.dma_start(k_win[t], k_rows[:, t, :])
+        nc.sync.dma_start(v_pair[:], vT[0 : 2 * P, :].rearrange("(m b) w -> m b w", b=2))
+        for b in range(2, BLOCKS):
+            nc.sync.dma_start(v_win[b], vT[b * P : (b + 1) * P, :])
 
         ident = keep.tile([P, P], F32, name="ident")
         make_identity(nc, ident[:])
@@ -73,7 +78,7 @@ def tile_attend_rbf_topk_kernel(tc, qT, kT, vT, vs, kb, offs, out):
         v_codes = {}
 
         def gather_values(b):
-            nc.vector.tensor_copy(v_sb[b][:].rearrange("p (u m h) -> p m u h", u=PAIRS, h=2), v_win[b][:].indirect(offsets[:]))
+            nc.vector.tensor_copy(v_sb[b][:].rearrange("p (u m h) -> p m u h", u=PAIRS, h=2), v_win[b].indirect(offsets[:]))
 
         def turn_values(b, pieces=1):
             words = v_sb[b][:].bitcast(F32)
@@ -98,7 +103,6 @@ def tile_attend_rbf_topk_kernel(tc, qT, kT, vT, vs, kb, offs, out):
 
         k_grouped = keep.tile([P, SLOTS, PACK], BF16, name="k_grouped", align_bytes=64)
         k_first = keep.tile([P, 2, SLOTS], F32, name="k_first")
-        nc.vector.tensor_copy(k_first[:, 0, :], k_win[0][:].indirect(offsets[:]))
 
         kb_row = keep.tile([P, SLOTS], F32, name="kb_row")
         nc.vector.tensor_copy(kb_row[:], kb_win[:].indirect(offsets[:]))
@@ -121,7 +125,8 @@ def tile_attend_rbf_topk_kernel(tc, qT, kT, vT, vs, kb, offs, out):
 
         nc.vector.quantize_mx(out=q_codes[:].bitcast(FP8X4), scales=q_scales[:], in_=q_grouped[:].rearrange("p q t -> p (q t)"))
 
-        nc.vector.tensor_copy(k_first[:, 1, :], k_win[1][:].indirect(offsets[:]))
+        for t in range(2):
+            nc.vector.tensor_copy(k_first[:, t, :], k_win[t].indirect(offsets[:]))
         nc.scalar.copy(k_grouped[:, :, 0:2], k_first[:].rearrange("p t i -> p i t"))
         kb_all = keep.tile([P, SLOTS], F32, name="kb_all")
         nc.scalar.copy(kb_all[:], kb_spread[:].rearrange("p c i -> p (c i)"))
@@ -137,11 +142,11 @@ def tile_attend_rbf_topk_kernel(tc, qT, kT, vT, vs, kb, offs, out):
         vs_all = keep.tile([P, SLOTS], F32, name="vs_all")
         nc.scalar.copy(vs_all[:], vs_spread[:].rearrange("p c i -> p (c i)"))
 
-        nc.vector.tensor_copy(k_grouped[:, :, 2], k_win[2][:].indirect(offsets[:]))
+        nc.vector.tensor_copy(k_grouped[:, :, 2], k_win[2].indirect(offsets[:]))
         halves = [slice(h * HALF, (h + 1) * HALF) for h in range(2)]
         for h in range(2):
             listed = offsets[:, h * (HALF // 16) : (h + 1) * (HALF // 16)]
-            nc.vector.tensor_copy(k_grouped[:, halves[h], 3], k_win[3][:].indirect(listed))
+            nc.vector.tensor_copy(k_grouped[:, halves[h], 3], k_win[3].indirect(listed))
         k_codes = keep.tile([P, SLOTS], U32, name="k_codes", align_bytes=64)
         k_scales = keep.tile([P, SLOTS], U8, name="k_scales", align_bytes=64)
         score = [psum.tile([NQ, HALF], F32, name=f"score{h}", tag="score", bufs=2) for h in range(2)]
@@ -218,9 +223,9 @@ def tile_attend_rbf_topk_kernel(tc, qT, kT, vT, vs, kb, offs, out):
         y_first = psum.tile([NQ, 2, P], F32, name="y_first", tag="y")
         for b in range(2):
             product(y_first[:, b, :], b)
-        out_first = keep.tile([NQ, 2 * P], F32, name="out_first")
-        nc.scalar.activation(out_first[:], y_first[:].rearrange("q b e -> q (b e)"), copy, scale=inverse[:])
-        nc.sync.dma_start(out[0, :, 0 : 2 * P], out_first[:])
+        out_first = keep.tile([NQ, P, 2], F32, name="out_first")
+        nc.scalar.activation(out_first[:], y_first[:].rearrange("q b e -> q e b"), copy, scale=inverse[:])
+        nc.sync.dma_start(out[0, :, 0 : 2 * P], out_first[:].rearrange("q e b -> q (e b)"))
 
         y_next = psum.tile([NQ, P], F32, name="y_next", tag="y")
         product(y_next[:], 2)

@@ -23,6 +23,7 @@ KB_ROW = P - 1
 VS_ROW = P // 2 - 1
 WINDOW_BYTES = 4 * POOL
 HALF = SLOTS // 2
+BANK = 2048
 COLS = SLOTS // P
 
 FLOPS = 2 * NQ * SLOTS * (D + DV)
@@ -38,7 +39,7 @@ def tile_attend_rbf_topk_kernel(tc, qT, kT, vT, vs, kb, offs, out):
     with ExitStack() as ctx:
         keep = ctx.enter_context(tc.tile_pool(name="keep", bufs=1))
         over = ctx.enter_context(tc.tile_pool(name="over", bufs=1))
-        psum = ctx.enter_context(tc.psum_pool(name="psum", bufs=2))
+        psum = ctx.enter_context(tc.psum_pool(name="psum", bufs=1))
 
         offsets = keep.tile([P, SLOTS // 16], U16, name="offsets")
 
@@ -82,7 +83,7 @@ def tile_attend_rbf_topk_kernel(tc, qT, kT, vT, vs, kb, offs, out):
 
         def turn_values(b, pieces=1):
             words = v_sb[b][:].bitcast(F32)
-            v_turn = psum.tile([P, PAIRS, P], F32, name=f"v_turn{b}", tag="v_turn", bufs=2)
+            v_turn = psum.tile([P, PAIRS, P], F32, name=f"v_turn{b}", offset=b * BANK)
             for u in range(PAIRS):
                 nc.tensor.transpose(v_turn[:, u, :], words[:, u * P : (u + 1) * P], ident[:])
             for j in range(pieces):
@@ -114,12 +115,12 @@ def tile_attend_rbf_topk_kernel(tc, qT, kT, vT, vs, kb, offs, out):
         q_scales = keep.tile([P, NQ], U8, name="q_scales", align_bytes=64)
         nc.scalar.copy(q_grouped[:], q_raw[:].rearrange("p t q -> p q t"))
 
-        kb_turn = psum.tile([P, COLS, P], F32, name="kb_turn", tag="turn")
+        kb_turn = psum.tile([P, COLS, P], F32, name="kb_turn", offset=0)
         for c in range(COLS):
             nc.tensor.transpose(kb_turn[:, c, :], kb_row[:, c * P : (c + 1) * P], ident[:])
         kb_col = keep.tile([P, COLS], F32, name="kb_col")
         nc.scalar.copy(kb_col[:], kb_turn[:, :, KB_ROW])
-        kb_spread = psum.tile([P, COLS, P], F32, name="kb_spread", tag="turn")
+        kb_spread = psum.tile([P, COLS, P], F32, name="kb_spread", offset=BANK)
         for c in range(COLS):
             nc.tensor.transpose(kb_spread[:, c, :], kb_col[:, c : c + 1].to_broadcast([P, P]), ident[:])
 
@@ -131,12 +132,12 @@ def tile_attend_rbf_topk_kernel(tc, qT, kT, vT, vs, kb, offs, out):
         kb_all = keep.tile([P, SLOTS], F32, name="kb_all")
         nc.scalar.copy(kb_all[:], kb_spread[:].rearrange("p c i -> p (c i)"))
 
-        vs_turn = psum.tile([P, COLS, P], F32, name="vs_turn", tag="turn")
+        vs_turn = psum.tile([P, COLS, P], F32, name="vs_turn", offset=2 * BANK)
         for c in range(COLS):
             nc.tensor.transpose(vs_turn[:, c, :], vs_row[:, c * P : (c + 1) * P], ident[:])
         vs_col = keep.tile([P, COLS], F32, name="vs_col")
         nc.scalar.copy(vs_col[:], vs_turn[:, :, VS_ROW])
-        vs_spread = psum.tile([P, COLS, P], F32, name="vs_spread", tag="turn")
+        vs_spread = psum.tile([P, COLS, P], F32, name="vs_spread", offset=3 * BANK)
         for c in range(COLS):
             nc.tensor.transpose(vs_spread[:, c, :], vs_col[:, c : c + 1].to_broadcast([P, P]), ident[:])
         vs_all = keep.tile([P, SLOTS], F32, name="vs_all")
@@ -149,7 +150,7 @@ def tile_attend_rbf_topk_kernel(tc, qT, kT, vT, vs, kb, offs, out):
             nc.vector.tensor_copy(k_grouped[:, halves[h], 3], k_win[3].indirect(listed))
         k_codes = keep.tile([P, SLOTS], U32, name="k_codes", align_bytes=64)
         k_scales = keep.tile([P, SLOTS], U8, name="k_scales", align_bytes=64)
-        score = [psum.tile([NQ, HALF], F32, name=f"score{h}", tag="score", bufs=2) for h in range(2)]
+        score = [psum.tile([NQ, HALF], F32, name=f"score{h}", offset=(4 + h) * BANK) for h in range(2)]
         for h in range(2):
             nc.vector.quantize_mx(
                 out=k_codes[:, halves[h]].bitcast(FP8X4),
@@ -178,7 +179,7 @@ def tile_attend_rbf_topk_kernel(tc, qT, kT, vT, vs, kb, offs, out):
 
         w_sb = keep.tile([NQ, SLOTS], BF16, name="w_sb")
         nc.gpsimd.tensor_tensor(w_sb[:], p[:], vs_all[:], mult)
-        w_turn = psum.tile([P, PAIRS, NQ], F32, name="w_turn", tag="turn")
+        w_turn = psum.tile([P, PAIRS, NQ], F32, name="w_turn", offset=7 * BANK)
         for u in range(PAIRS):
             nc.tensor.transpose(w_turn[:, u, :], w_sb[:].bitcast(F32)[:, u : PAIRS * P : PAIRS], ident[:])
         w_grouped = keep.tile([P, NQ, PACK], BF16, name="w_grouped", align_bytes=64)
@@ -191,13 +192,13 @@ def tile_attend_rbf_topk_kernel(tc, qT, kT, vT, vs, kb, offs, out):
             turn_values(b)
         inverse = over.tile([NQ, 1], F32, name="inverse", offset=2 * WINDOW_BYTES, align_bytes=64)
         nc.vector.reciprocal(inverse[:], total[:])
-        gather_values(3)
-        codes_01 = over.tile([P, 2 * P], U32, name="codes_01", offset=3 * WINDOW_BYTES, align_bytes=64)
-        codes_2 = over.tile([P, P], U32, name="codes_2", offset=3 * WINDOW_BYTES + 4 * 3 * P, align_bytes=64)
-        w_codes = over.tile([P, NQ], U32, name="w_codes", offset=3 * WINDOW_BYTES + 4 * 2 * P, align_bytes=64)
-        quantize_values(0, 2, codes_01[:])
+        w_codes = over.tile([P, NQ], U32, name="w_codes", offset=2 * WINDOW_BYTES + 64, align_bytes=64)
         w_scales = keep.tile([P, NQ], U8, name="w_scales", align_bytes=64)
         nc.vector.quantize_mx(out=w_codes[:].bitcast(FP8X4), scales=w_scales[:], in_=w_grouped[:].rearrange("p q t -> p (q t)"))
+        gather_values(3)
+        codes_01 = over.tile([P, 2 * P], U32, name="codes_01", offset=3 * WINDOW_BYTES, align_bytes=64)
+        codes_2 = over.tile([P, P], U32, name="codes_2", offset=3 * WINDOW_BYTES + 4 * 2 * P, align_bytes=64)
+        quantize_values(0, 2, codes_01[:])
         quantize_values(2, 1, codes_2[:])
         turn_values(3, pieces=2)
         codes_3 = keep.tile([P, P], U32, name="codes_3", align_bytes=64)
@@ -220,21 +221,28 @@ def tile_attend_rbf_topk_kernel(tc, qT, kT, vT, vs, kb, offs, out):
                 stop=True,
             )
 
-        y_first = psum.tile([NQ, 2, P], F32, name="y_first", tag="y")
-        for b in range(2):
-            product(y_first[:, b, :], b)
+        y_first = psum.tile([NQ, 2, P], F32, name="y_first", offset=6 * BANK)
+        nc.tensor.matmul_mx(
+            out=y_first[:].rearrange("q b e -> q (b e)"),
+            lhsT=w_codes[:].bitcast(FP8X4),
+            lhsT_scale=w_scales[:],
+            rhs=codes_01[:].bitcast(FP8X4),
+            rhs_scale=v_scales[:, 0:2, :].rearrange("p b e -> p (b e)"),
+            start=True,
+            stop=True,
+        )
         out_first = keep.tile([NQ, P, 2], F32, name="out_first")
         nc.scalar.activation(out_first[:], y_first[:].rearrange("q b e -> q e b"), copy, scale=inverse[:])
         nc.sync.dma_start(out[0, :, 0 : 2 * P], out_first[:].rearrange("q e b -> q (e b)"))
 
-        y_next = psum.tile([NQ, P], F32, name="y_next", tag="y")
+        y_next = psum.tile([NQ, P], F32, name="y_next", offset=7 * BANK)
         product(y_next[:], 2)
         out_next = keep.tile([NQ, P], F32, name="out_next")
         nc.scalar.activation(out_next[:], y_next[:], copy, scale=inverse[:])
         nc.sync.dma_start(out[0, :, 2 * P : 3 * P], out_next[:])
 
         out_last = keep.tile([NQ, P], F32, name="out_last")
-        y_last = [psum.tile([NQ, P // 2], F32, name=f"y_last{j}", tag="score", bufs=2) for j in range(2)]
+        y_last = [psum.tile([NQ, P // 2], F32, name=f"y_last{j}", offset=(4 + j) * BANK) for j in range(2)]
         for j, part in enumerate(parts):
             nc.tensor.matmul_mx(
                 out=y_last[j][:],

@@ -70,9 +70,6 @@ def tile_attend_rbf_topk_kernel(tc, qT, kT, vT, vs, kb, offs, out):
         nc.vector.memset(vs_win[0:VS_ROW, :], 0.0)
         nc.gpsimd.memset(vs_win[VS_ROW + 1 : P, :], 0.0)
 
-        warm = keep.tile([P, 1], F32, name="warm")
-        nc.scalar.activation(warm[:], ident[:, 0:1], exp)
-
         v_scales = keep.tile([P, BLOCKS, P], U8, name="v_scales", align_bytes=64)
         v_sb = [keep.tile([P, SLOTS], BF16, name=f"v_sb{b}") for b in range(BLOCKS)]
         v_grouped = keep.tile([P, BLOCKS, P, PACK], BF16, name="v_grouped", align_bytes=64)

@@ -131,14 +131,9 @@ def tile_attend_rbf_topk_kernel(tc, qT, kT, vT, vs, kb, offs, out):
 
         vs_turn = psum.tile([P, COLS, P], F32, name="vs_turn", offset=2 * BANK)
         for c in range(COLS):
-            nc.tensor.transpose(vs_turn[:, c, :], vs_row[:, c * P : (c + 1) * P], ident[:])
+            nc.tensor.transpose(vs_turn[:, c, :], vs_row[:, c:SLOTS:PACK], ident[:])
         vs_col = keep.tile([P, COLS], F32, name="vs_col")
         nc.scalar.copy(vs_col[:], vs_turn[:, :, VS_ROW])
-        vs_spread = psum.tile([P, COLS, P], F32, name="vs_spread", offset=3 * BANK)
-        for c in range(COLS):
-            nc.tensor.transpose(vs_spread[:, c, :], vs_col[:, c : c + 1].to_broadcast([P, P]), ident[:])
-        vs_all = keep.tile([P, SLOTS], F32, name="vs_all")
-        nc.scalar.copy(vs_all[:], vs_spread[:].rearrange("p c i -> p (c i)"))
 
         nc.vector.tensor_copy(k_grouped[:, :, 2], k_win[2].indirect(offsets[:]))
         halves = [slice(h * HALF, (h + 1) * HALF) for h in range(2)]
@@ -172,18 +167,23 @@ def tile_attend_rbf_topk_kernel(tc, qT, kT, vT, vs, kb, offs, out):
 
         p = keep.tile([NQ, SLOTS], F32, name="p")
         total = keep.tile([NQ, 1], F32, name="total")
-        nc.scalar.activation(p[:], neg[:], exp, bias=neg_m[:], scale=-1.0, accum_out=total[:])
-
-        w_sb = keep.tile([NQ, SLOTS], BF16, name="w_sb")
-        nc.gpsimd.tensor_tensor(w_sb[:], p[:], vs_all[:], mult)
-        w_turn = psum.tile([P, PAIRS, NQ], F32, name="w_turn", offset=7 * BANK)
-        for u in range(PAIRS):
-            nc.tensor.transpose(w_turn[:, u, :], w_sb[:].bitcast(F32)[:, u : PAIRS * P : PAIRS], ident[:])
-        w_grouped = keep.tile([P, NQ, PACK], BF16, name="w_grouped", align_bytes=64)
-        nc.scalar.copy(
-            w_grouped[:].rearrange("p q t -> p (q t)").bitcast(F32).rearrange("p (q u) -> p q u", u=PAIRS),
-            w_turn[:].rearrange("p u q -> p q u"),
+        nc.scalar.activation(
+            p[:].rearrange("q (t m) -> q m t", t=PACK),
+            neg[:].rearrange("q (m t) -> q m t", t=PACK),
+            exp,
+            bias=neg_m[:],
+            scale=-1.0,
+            accum_out=total[:],
         )
+
+        p_turn = psum.tile([P, PACK, NQ], F32, name="p_turn", offset=7 * BANK)
+        for t in range(PACK):
+            nc.tensor.transpose(p_turn[:, t, :], p[:, t * P : (t + 1) * P], ident[:])
+        w_planes = keep.tile([P, PACK, NQ], BF16, name="w_planes")
+        for t in range(PACK):
+            nc.scalar.activation(w_planes[:, t, :], p_turn[:, t, :], copy, scale=vs_col[:, t : t + 1])
+        w_grouped = keep.tile([P, NQ, PACK], BF16, name="w_grouped", align_bytes=64)
+        nc.scalar.copy(w_grouped[:], w_planes[:].rearrange("p t q -> p q t"))
         for b in range(BLOCKS - 1):
             gather_values(b)
             turn_values(b)

@@ -78,17 +78,20 @@ def tile_attend_rbf_topk_kernel(tc, qT, kT, vT, vs, kb, offs, out):
         def gather_values(b):
             nc.vector.tensor_copy(v_sb[b][:].rearrange("p (u m h) -> p m u h", u=PAIRS, h=2), v_win[b].indirect(offsets[:]))
 
+        def grouped_words(b):
+            words = v_grouped[:].rearrange("p b e t -> p (b e t)").bitcast(F32)
+            if b < 2:
+                return words[:, 0 : 2 * PAIRS * P].rearrange("p (j b e u) -> p b j e u", j=2, b=2, u=PAIRS)[:, b]
+            return words[:, b * PAIRS * P : (b + 1) * PAIRS * P].rearrange("p (j e u) -> p j e u", j=2, u=PAIRS)
+
         def turn_values(b, pieces=1):
             words = v_sb[b][:].bitcast(F32)
             v_turn = psum.tile([P, PAIRS, P], F32, name=f"v_turn{b}", offset=b * BANK)
             for u in range(PAIRS):
                 nc.tensor.transpose(v_turn[:, u, :], words[:, u * P : (u + 1) * P], ident[:])
             for j in range(pieces):
-                part = slice(j * P // pieces, (j + 1) * P // pieces)
-                nc.scalar.copy(
-                    v_grouped[:, b, part].rearrange("p e t -> p (e t)").bitcast(F32).rearrange("p (e u) -> p e u", u=PAIRS),
-                    v_turn[:, :, part].rearrange("p u e -> p e u"),
-                )
+                part = slice(j * 2 // pieces, (j + 1) * 2 // pieces)
+                nc.scalar.copy(grouped_words(b)[:, part], v_turn[:].rearrange("p u (j e) -> p j e u", j=2)[:, part])
 
         def quantize_values(first, count, codes):
             nc.vector.quantize_mx(
@@ -193,10 +196,9 @@ def tile_attend_rbf_topk_kernel(tc, qT, kT, vT, vs, kb, offs, out):
         w_scales = keep.tile([P, NQ], U8, name="w_scales", align_bytes=64)
         nc.vector.quantize_mx(out=w_codes[:].bitcast(FP8X4), scales=w_scales[:], in_=w_grouped[:].rearrange("p q t -> p (q t)"))
         gather_values(3)
-        codes_01 = over.tile([P, 2 * P], U32, name="codes_01", offset=3 * WINDOW_BYTES, align_bytes=64)
-        codes_2 = over.tile([P, P], U32, name="codes_2", offset=3 * WINDOW_BYTES + 4 * 2 * P, align_bytes=64)
-        quantize_values(0, 2, codes_01[:])
-        quantize_values(2, 1, codes_2[:])
+        for b in range(BLOCKS - 1):
+            codes = over.tile([P, P], U32, name=f"codes_{b}", offset=3 * WINDOW_BYTES + 4 * P * b, align_bytes=64)
+            quantize_values(b, 1, codes[:])
         turn_values(3, pieces=2)
         codes_3 = keep.tile([P, P], U32, name="codes_3", align_bytes=64)
         parts = [slice(j * P // 2, (j + 1) * P // 2) for j in range(2)]
@@ -218,19 +220,12 @@ def tile_attend_rbf_topk_kernel(tc, qT, kT, vT, vs, kb, offs, out):
                 stop=True,
             )
 
-        y_first = psum.tile([NQ, 2, P], F32, name="y_first", offset=6 * BANK)
-        nc.tensor.matmul_mx(
-            out=y_first[:].rearrange("q b e -> q (b e)"),
-            lhsT=w_codes[:].bitcast(FP8X4),
-            lhsT_scale=w_scales[:],
-            rhs=codes_01[:].bitcast(FP8X4),
-            rhs_scale=v_scales[:, 0:2, :].rearrange("p b e -> p (b e)"),
-            start=True,
-            stop=True,
-        )
-        out_first = keep.tile([NQ, P, 2], F32, name="out_first")
-        nc.scalar.activation(out_first[:], y_first[:].rearrange("q b e -> q e b"), copy, scale=inverse[:])
-        nc.sync.dma_start(out[0, :, 0 : 2 * P], out_first[:].rearrange("q e b -> q (e b)"))
+        for j, bank in enumerate((6, 0)):
+            y_first = psum.tile([NQ, P], F32, name=f"y_first{j}", offset=bank * BANK)
+            product(y_first[:], j)
+            out_first = keep.tile([NQ, P // 2, 2], F32, name=f"out_first{j}")
+            nc.scalar.activation(out_first[:], y_first[:].rearrange("q (b e) -> q e b", b=2), copy, scale=inverse[:])
+            nc.sync.dma_start(out[0, :, j * P : (j + 1) * P], out_first[:].rearrange("q e b -> q (e b)"))
 
         y_next = psum.tile([NQ, P], F32, name="y_next", offset=7 * BANK)
         product(y_next[:], 2)

@@ -55,8 +55,8 @@ def tile_attend_rbf_topk_kernel(tc, qT, kT, vT, vs, kb, offs, out):
         vs_win = keep.tile([P, POOL], F32, name="vs_win")
         nc.sync.dma_start(q_raw[:], qT[0].rearrange("(m t) q -> m t q", t=PACK))
         nc.sync.dma_start(offsets[:], offs)
-        nc.sync.dma_start(kb_win[KB_ROW : KB_ROW + 1, :], kb[0:1, :])
-        nc.sync.dma_start(vs_win[VS_ROW : VS_ROW + 1, :], vs[0:1, :])
+        nc.scalar.dma_start(kb_win[KB_ROW : KB_ROW + 1, :], kb[0:1, :])
+        nc.scalar.dma_start(vs_win[VS_ROW : VS_ROW + 1, :], vs[0:1, :])
         nc.sync.dma_start(k_pair[:], k_rows[:, 0:2, :])
         for t in range(2, PACK):
             nc.sync.dma_start(k_win[t], k_rows[:, t, :])
@@ -179,12 +179,11 @@ def tile_attend_rbf_topk_kernel(tc, qT, kT, vT, vs, kb, offs, out):
             accum_out=total[:],
         )
 
-        p_turn = psum.tile([P, PACK, NQ], F32, name="p_turn", offset=7 * BANK)
-        for t in range(PACK):
-            nc.tensor.transpose(p_turn[:, t, :], p[:, t * P : (t + 1) * P], ident[:])
+        p_turn = [psum.tile([P, NQ], F32, name=f"p_turn{t}", offset=(4 + t) * BANK) for t in range(PACK)]
         w_planes = keep.tile([P, PACK, NQ], BF16, name="w_planes")
         for t in range(PACK):
-            nc.scalar.activation(w_planes[:, t, :], p_turn[:, t, :], copy, scale=vs_col[:, t : t + 1])
+            nc.tensor.transpose(p_turn[t][:], p[:, t * P : (t + 1) * P], ident[:])
+            nc.scalar.activation(w_planes[:, t, :], p_turn[t][:], copy, scale=vs_col[:, t : t + 1])
         w_grouped = keep.tile([P, NQ, PACK], BF16, name="w_grouped", align_bytes=64)
         nc.scalar.copy(w_grouped[:], w_planes[:].rearrange("p t q -> p q t"))
         for b in range(BLOCKS - 1):

@@ -18,16 +18,18 @@ D = 512
 DV = 512
 PACK = 4
 PAIRS = 2
-BLOCKS = DV // P
+PER_COLUMN = 16
 KB_ROW = P - 1
 VS_ROW = P // 2 - 1
 WINDOW_BYTES = 4 * POOL
+SPARE = 5 * WINDOW_BYTES
 HALF = SLOTS // 2
+SHARE = 256
 BANK = 2048
 COLS = SLOTS // P
 
 FLOPS = 2 * NQ * SLOTS * (D + DV)
-BYTES = 4 * ((D + DV) * POOL + 2 * POOL + D * NQ + NQ * DV) + 2 * P * (SLOTS // 16)
+BYTES = 4 * ((D + DV) * POOL + 2 * POOL + D * NQ + NQ * DV) + 2 * P * (SLOTS // PER_COLUMN)
 
 
 def tile_attend_rbf_topk_kernel(tc, qT, kT, vT, vs, kb, offs, out):
@@ -41,15 +43,25 @@ def tile_attend_rbf_topk_kernel(tc, qT, kT, vT, vs, kb, offs, out):
         over = ctx.enter_context(tc.tile_pool(name="over", bufs=1))
         psum = ctx.enter_context(tc.psum_pool(name="psum", bufs=1))
 
-        offsets = keep.tile([P, SLOTS // 16], U16, name="offsets")
+        def reuse(name, shape, dtype, offset):
+            return over.tile(shape, dtype, name=name, offset=offset, align_bytes=64)
+
+        def bank(name, shape, number):
+            return psum.tile(shape, F32, name=name, offset=number * BANK)
+
+        offsets = keep.tile([P, SLOTS // PER_COLUMN], U16, name="offsets")
+
+        def listed(first, last):
+            return offsets[:, first // PER_COLUMN : last // PER_COLUMN]
 
         k_rows = kT.rearrange("(m t) w -> m t w", t=PACK)
         k_pair = keep.tile([P, 2, POOL], F32, name="k_pair")
-        k_rest = [keep.tile([P, POOL], F32, name=f"k_win{t}") for t in range(2, PACK)]
-        k_win = [k_pair[:, 0, :], k_pair[:, 1, :], k_rest[0][:], k_rest[1][:]]
-        v_pair = over.tile([P, 2, POOL], F32, name="v_pair", offset=0, align_bytes=64)
-        v_rest = [over.tile([P, POOL], F32, name=f"v_win{b}", offset=b * WINDOW_BYTES, align_bytes=64) for b in range(2, BLOCKS)]
-        v_win = [v_pair[:, 0, :], v_pair[:, 1, :], v_rest[0][:], v_rest[1][:]]
+        k_two = keep.tile([P, POOL], F32, name="k_two")
+        k_three = reuse("k_three", [P, POOL], F32, 4 * WINDOW_BYTES)
+        v_zero = reuse("v_zero", [P, POOL], F32, 0)
+        v_one = reuse("v_one", [P, POOL], F32, WINDOW_BYTES)
+        v_two = reuse("v_two", [P, POOL], F32, 2 * WINDOW_BYTES)
+        v_three = reuse("v_three", [P, POOL], F32, 3 * WINDOW_BYTES)
         q_raw = keep.tile([P, PACK, NQ], F32, name="q_raw")
         kb_win = keep.tile([P, POOL], F32, name="kb_win")
         vs_win = keep.tile([P, POOL], F32, name="vs_win")
@@ -58,52 +70,18 @@ def tile_attend_rbf_topk_kernel(tc, qT, kT, vT, vs, kb, offs, out):
         nc.scalar.dma_start(kb_win[KB_ROW : KB_ROW + 1, :], kb[0:1, :])
         nc.scalar.dma_start(vs_win[VS_ROW : VS_ROW + 1, :], vs[0:1, :])
         nc.sync.dma_start(k_pair[:], k_rows[:, 0:2, :])
-        for t in range(2, PACK):
-            nc.sync.dma_start(k_win[t], k_rows[:, t, :])
-        nc.sync.dma_start(v_pair[:], vT[0 : 2 * P, :].rearrange("(m b) w -> m b w", b=2))
-        for b in range(2, BLOCKS):
-            nc.sync.dma_start(v_win[b], vT[b * P : (b + 1) * P, :])
+        nc.sync.dma_start(k_two[:], k_rows[:, 2, :])
+        nc.sync.dma_start(k_three[:], k_rows[:, 3, :])
+        nc.sync.dma_start(v_zero[:], vT[0:P, :])
+        nc.sync.dma_start(v_one[:], vT[P : 2 * P, :])
+        nc.sync.dma_start(v_two[:], vT[2 * P : 3 * P, :])
+        nc.sync.dma_start(v_three[:], vT[3 * P : DV, :])
 
         ident = keep.tile([P, P], F32, name="ident")
         make_identity(nc, ident[:])
         nc.vector.memset(kb_win[0:KB_ROW, :], 0.0)
         nc.vector.memset(vs_win[0:VS_ROW, :], 0.0)
         nc.gpsimd.memset(vs_win[VS_ROW + 1 : P, :], 0.0)
-
-        v_scales = keep.tile([P, BLOCKS, P], U8, name="v_scales", align_bytes=64)
-        v_sb = [keep.tile([P, SLOTS], BF16, name=f"v_sb{b}") for b in range(BLOCKS)]
-        v_grouped = keep.tile([P, BLOCKS, P, PACK], BF16, name="v_grouped", align_bytes=64)
-        v_codes = {}
-
-        def gather_values(b):
-            nc.vector.tensor_copy(v_sb[b][:].rearrange("p (u m h) -> p m u h", u=PAIRS, h=2), v_win[b].indirect(offsets[:]))
-
-        def grouped_words(b):
-            words = v_grouped[:].rearrange("p b e t -> p (b e t)").bitcast(F32)
-            if b < 2:
-                return words[:, 0 : 2 * PAIRS * P].rearrange("p (j b e u) -> p b j e u", j=2, b=2, u=PAIRS)[:, b]
-            return words[:, b * PAIRS * P : (b + 1) * PAIRS * P].rearrange("p (j e u) -> p j e u", j=2, u=PAIRS)
-
-        def turn_values(b, pieces=1):
-            words = v_sb[b][:].bitcast(F32)
-            v_turn = psum.tile([P, PAIRS, P], F32, name=f"v_turn{b}", offset=b * BANK)
-            for u in range(PAIRS):
-                nc.tensor.transpose(v_turn[:, u, :], words[:, u * P : (u + 1) * P], ident[:])
-            for j in range(pieces):
-                part = slice(j * 2 // pieces, (j + 1) * 2 // pieces)
-                nc.scalar.copy(grouped_words(b)[:, part], v_turn[:].rearrange("p u (j e) -> p j e u", j=2)[:, part])
-
-        def quantize_values(first, count, codes):
-            nc.vector.quantize_mx(
-                out=codes.bitcast(FP8X4),
-                scales=v_scales[:, first : first + count, :].rearrange("p b e -> p (b e)"),
-                in_=v_grouped[:, first : first + count].rearrange("p b e t -> p (b e t)"),
-            )
-            for b in range(count):
-                v_codes[first + b] = codes[:, b * P : (b + 1) * P]
-
-        k_grouped = keep.tile([P, SLOTS, PACK], BF16, name="k_grouped", align_bytes=64)
-        k_first = keep.tile([P, 2, SLOTS], F32, name="k_first")
 
         kb_row = keep.tile([P, SLOTS], F32, name="kb_row")
         nc.vector.tensor_copy(kb_row[:], kb_win[:].indirect(offsets[:]))
@@ -114,38 +92,37 @@ def tile_attend_rbf_topk_kernel(tc, qT, kT, vT, vs, kb, offs, out):
         q_codes = keep.tile([P, NQ], U32, name="q_codes", align_bytes=64)
         q_scales = keep.tile([P, NQ], U8, name="q_scales", align_bytes=64)
         nc.scalar.copy(q_grouped[:], q_raw[:].rearrange("p t q -> p q t"))
+        nc.vector.quantize_mx(out=q_codes[:].bitcast(FP8X4), scales=q_scales[:], in_=q_grouped[:].rearrange("p q t -> p (q t)"))
 
-        kb_turn = psum.tile([P, COLS, P], F32, name="kb_turn", offset=0)
+        kb_turn = bank("kb_turn", [P, COLS, P], 0)
         for c in range(COLS):
             nc.tensor.transpose(kb_turn[:, c, :], kb_row[:, c * P : (c + 1) * P], ident[:])
         kb_col = keep.tile([P, COLS], F32, name="kb_col")
         nc.scalar.copy(kb_col[:], kb_turn[:, :, KB_ROW])
-        kb_spread = psum.tile([P, COLS, P], F32, name="kb_spread", offset=BANK)
+        kb_spread = bank("kb_spread", [P, COLS, P], 1)
         for c in range(COLS):
             nc.tensor.transpose(kb_spread[:, c, :], kb_col[:, c : c + 1].to_broadcast([P, P]), ident[:])
-
-        nc.vector.quantize_mx(out=q_codes[:].bitcast(FP8X4), scales=q_scales[:], in_=q_grouped[:].rearrange("p q t -> p (q t)"))
-
-        for t in range(2):
-            nc.vector.tensor_copy(k_first[:, t, :], k_win[t].indirect(offsets[:]))
-        nc.scalar.copy(k_grouped[:, :, 0:2], k_first[:].rearrange("p t i -> p i t"))
         kb_all = keep.tile([P, SLOTS], F32, name="kb_all")
         nc.scalar.copy(kb_all[:], kb_spread[:].rearrange("p c i -> p (c i)"))
 
-        vs_turn = psum.tile([P, COLS, P], F32, name="vs_turn", offset=2 * BANK)
-        for c in range(COLS):
-            nc.tensor.transpose(vs_turn[:, c, :], vs_row[:, c:SLOTS:PACK], ident[:])
-        vs_col = keep.tile([P, COLS], F32, name="vs_col")
+        vs_turn = bank("vs_turn", [P, PACK, P], 2)
+        for t in range(PACK):
+            nc.tensor.transpose(vs_turn[:, t, :], vs_row[:, t:SLOTS:PACK], ident[:])
+        vs_col = keep.tile([P, PACK], F32, name="vs_col")
         nc.scalar.copy(vs_col[:], vs_turn[:, :, VS_ROW])
 
-        nc.vector.tensor_copy(k_grouped[:, :, 2], k_win[2].indirect(offsets[:]))
+        k_grouped = keep.tile([P, SLOTS, PACK], BF16, name="k_grouped", align_bytes=64)
+        k_first = keep.tile([P, 2, SLOTS], F32, name="k_first")
+        for t in range(2):
+            nc.vector.tensor_copy(k_first[:, t, :], k_pair[:, t, :].indirect(offsets[:]))
+        nc.scalar.copy(k_grouped[:, :, 0:2], k_first[:].rearrange("p t i -> p i t"))
+        nc.vector.tensor_copy(k_grouped[:, :, 2], k_two[:].indirect(offsets[:]))
         halves = [slice(h * HALF, (h + 1) * HALF) for h in range(2)]
         for h in range(2):
-            listed = offsets[:, h * (HALF // 16) : (h + 1) * (HALF // 16)]
-            nc.vector.tensor_copy(k_grouped[:, halves[h], 3], k_win[3].indirect(listed))
+            nc.vector.tensor_copy(k_grouped[:, halves[h], 3], k_three[:].indirect(listed(h * HALF, (h + 1) * HALF)))
         k_codes = keep.tile([P, SLOTS], U32, name="k_codes", align_bytes=64)
         k_scales = keep.tile([P, SLOTS], U8, name="k_scales", align_bytes=64)
-        score = [psum.tile([NQ, HALF], F32, name=f"score{h}", offset=(4 + h) * BANK) for h in range(2)]
+        score = [bank(f"score{h}", [NQ, HALF], 4 + h) for h in range(2)]
         for h in range(2):
             nc.vector.quantize_mx(
                 out=k_codes[:, halves[h]].bitcast(FP8X4),
@@ -162,87 +139,121 @@ def tile_attend_rbf_topk_kernel(tc, qT, kT, vT, vs, kb, offs, out):
                 stop=True,
             )
 
-        neg = keep.tile([NQ, SLOTS], F32, name="neg")
+        neg = reuse("neg", [NQ, SLOTS], F32, SPARE)
         for h in range(2):
             nc.vector.scalar_tensor_tensor(neg[:, halves[h]], score[h][:], -1.0, kb_all[:, halves[h]], mult, subtract)
         neg_m = keep.tile([NQ, 1], F32, name="neg_m")
         nc.vector.tensor_reduce(neg_m[:], neg[:], axis=mybir.AxisListType.X, op=minimum)
 
-        p = keep.tile([NQ, SLOTS], F32, name="p")
+        g_zero = reuse("g_zero", [P, SLOTS], BF16, 4 * WINDOW_BYTES)
+        nc.scalar.activation(g_zero[:], v_zero[:].indirect(offsets[:]), copy)
+
+        p = reuse("p", [NQ, PACK, P], F32, 0)
         total = keep.tile([NQ, 1], F32, name="total")
         nc.scalar.activation(
-            p[:].rearrange("q (t m) -> q m t", t=PACK),
+            p[:].rearrange("q t m -> q m t"),
             neg[:].rearrange("q (m t) -> q m t", t=PACK),
             exp,
             bias=neg_m[:],
             scale=-1.0,
             accum_out=total[:],
         )
-
-        p_turn = [psum.tile([P, NQ], F32, name=f"p_turn{t}", offset=(4 + t) * BANK) for t in range(PACK)]
-        w_planes = keep.tile([P, PACK, NQ], BF16, name="w_planes")
+        p_turn = bank("p_turn", [P, PACK, NQ], 6)
         for t in range(PACK):
-            nc.tensor.transpose(p_turn[t][:], p[:, t * P : (t + 1) * P], ident[:])
-            nc.scalar.activation(w_planes[:, t, :], p_turn[t][:], copy, scale=vs_col[:, t : t + 1])
-        w_grouped = keep.tile([P, NQ, PACK], BF16, name="w_grouped", align_bytes=64)
-        nc.scalar.copy(w_grouped[:], w_planes[:].rearrange("p t q -> p q t"))
-        for b in range(BLOCKS - 1):
-            gather_values(b)
-            turn_values(b)
-        inverse = over.tile([NQ, 1], F32, name="inverse", offset=2 * WINDOW_BYTES, align_bytes=64)
-        nc.vector.reciprocal(inverse[:], total[:])
-        w_codes = over.tile([P, NQ], U32, name="w_codes", offset=2 * WINDOW_BYTES + 64, align_bytes=64)
-        w_scales = keep.tile([P, NQ], U8, name="w_scales", align_bytes=64)
-        nc.vector.quantize_mx(out=w_codes[:].bitcast(FP8X4), scales=w_scales[:], in_=w_grouped[:].rearrange("p q t -> p (q t)"))
-        gather_values(3)
-        for b in range(BLOCKS - 1):
-            codes = over.tile([P, P], U32, name=f"codes_{b}", offset=3 * WINDOW_BYTES + 4 * P * b, align_bytes=64)
-            quantize_values(b, 1, codes[:])
-        turn_values(3, pieces=2)
-        codes_3 = keep.tile([P, P], U32, name="codes_3", align_bytes=64)
-        parts = [slice(j * P // 2, (j + 1) * P // 2) for j in range(2)]
-        for part in parts:
-            nc.vector.quantize_mx(
-                out=codes_3[:, part].bitcast(FP8X4),
-                scales=v_scales[:, 3, part],
-                in_=v_grouped[:, 3, part].rearrange("p e t -> p (e t)"),
-            )
+            nc.tensor.transpose(p_turn[:, t, :], p[:, t, :], ident[:])
 
-        def product(y, b):
+        def turn(name, pair_words, number):
+            turned = bank(name, [P, PAIRS, P], number)
+            for u in range(PAIRS):
+                nc.tensor.transpose(turned[:, u, :], pair_words(u), ident[:])
+            return turned
+
+        def in_order(gathered):
+            words = gathered[:].bitcast(F32)
+            return lambda u: words[:, u : SLOTS // 2 : PAIRS]
+
+        def lay(grouped, turned, move=nc.scalar.copy):
+            move(grouped.bitcast(F32).rearrange("p (e u) -> p e u", u=PAIRS), turned.rearrange("p u e -> p e u"))
+
+        def quantize(codes, scales, grouped):
+            nc.vector.quantize_mx(out=codes.bitcast(FP8X4), scales=scales, in_=grouped)
+
+        def gather_shared(gathered, window):
+            nc.vector.tensor_copy(gathered[:, 0:SHARE], window[:].indirect(listed(0, SHARE)))
+            nc.scalar.activation(gathered[:, SHARE:SLOTS], window[:].indirect(listed(SHARE, SLOTS)), copy)
+
+        g_one = keep.tile([P, SLOTS], BF16, name="g_one")
+        nc.vector.tensor_copy(g_one[:], v_one[:].indirect(offsets[:]))
+        turned_zero = turn("turned_zero", in_order(g_zero), 5)
+        turned_one = turn("turned_one", in_order(g_one), 1)
+
+        w_grouped = reuse("w_grouped", [P, NQ, PACK], BF16, WINDOW_BYTES)
+        nc.vector.tensor_tensor(
+            w_grouped[:], p_turn[:].rearrange("p t q -> p q t"), vs_col[:].unsqueeze(1).to_broadcast([P, NQ, PACK]), mult
+        )
+        inverse = reuse("inverse", [NQ, 1], F32, WINDOW_BYTES + 2 * NQ * PACK)
+        nc.vector.reciprocal(inverse[:], total[:])
+
+        pair_grouped = reuse("pair_grouped", [P, 2, P * PACK], BF16, SPARE + 2 * SLOTS)
+        lay(pair_grouped[:, 0, :], turned_zero[:])
+        lay(pair_grouped[:, 1, :], turned_one[:], nc.vector.tensor_copy)
+
+        g_two = reuse("g_two", [P, SLOTS], BF16, SPARE)
+        nc.scalar.activation(g_two[:], v_two[:].indirect(offsets[:]), copy)
+        turned_two = turn("turned_two", in_order(g_two), 2)
+
+        w_codes = keep.tile([P, NQ], U32, name="w_codes", align_bytes=64)
+        w_scales = keep.tile([P, NQ], U8, name="w_scales", align_bytes=64)
+        quantize(w_codes[:], w_scales[:], w_grouped[:].rearrange("p q t -> p (q t)"))
+        pair_codes = keep.tile([P, 2 * P], U32, name="pair_codes", align_bytes=64)
+        pair_scales = keep.tile([P, 2 * P], U8, name="pair_scales", align_bytes=64)
+        quantize(pair_codes[:], pair_scales[:], pair_grouped[:].rearrange("p b x -> p (b x)"))
+
+        def product(y, codes, scales):
             nc.tensor.matmul_mx(
                 out=y,
                 lhsT=w_codes[:].bitcast(FP8X4),
                 lhsT_scale=w_scales[:],
-                rhs=v_codes[b].bitcast(FP8X4),
-                rhs_scale=v_scales[:, b, :],
+                rhs=codes.bitcast(FP8X4),
+                rhs_scale=scales,
                 start=True,
                 stop=True,
             )
 
-        for j, bank in enumerate((6, 0)):
-            y_first = psum.tile([NQ, P], F32, name=f"y_first{j}", offset=bank * BANK)
-            product(y_first[:], j)
-            out_first = keep.tile([NQ, P // 2, 2], F32, name=f"out_first{j}")
-            nc.scalar.activation(out_first[:], y_first[:].rearrange("q (b e) -> q e b", b=2), copy, scale=inverse[:])
-            nc.sync.dma_start(out[0, :, j * P : (j + 1) * P], out_first[:].rearrange("q e b -> q (e b)"))
+        y_pair = bank("y_pair", [NQ, 2 * P], 0)
+        product(y_pair[:], pair_codes[:], pair_scales[:])
 
-        y_next = psum.tile([NQ, P], F32, name="y_next", offset=7 * BANK)
-        product(y_next[:], 2)
-        out_next = keep.tile([NQ, P], F32, name="out_next")
-        nc.scalar.activation(out_next[:], y_next[:], copy, scale=inverse[:])
-        nc.sync.dma_start(out[0, :, 2 * P : 3 * P], out_next[:])
+        g_three = reuse("g_three", [P, SLOTS], BF16, SPARE + 4 * SLOTS)
+        gather_shared(g_three, v_three)
+        turned_three = turn("turned_three", in_order(g_three), 3)
 
-        out_last = keep.tile([NQ, P], F32, name="out_last")
-        y_last = [psum.tile([NQ, P // 2], F32, name=f"y_last{j}", offset=(4 + j) * BANK) for j in range(2)]
+        two_grouped = reuse("two_grouped", [P, P * PACK], BF16, 3 * WINDOW_BYTES)
+        lay(two_grouped[:], turned_two[:])
+        two_codes = keep.tile([P, P], U32, name="two_codes", align_bytes=64)
+        two_scales = keep.tile([P, P], U8, name="two_scales", align_bytes=64)
+        out_pair = reuse("out_pair", [NQ, 2 * P], F32, 3 * WINDOW_BYTES + 2 * P * PACK)
+        nc.vector.tensor_scalar(out_pair[:], y_pair[:], inverse[:], None, mult)
+        nc.sync.dma_start(out[0, :, 0 : 2 * P], out_pair[:])
+
+        quantize(two_codes[:], two_scales[:], two_grouped[:])
+        three_grouped = keep.tile([P, P * PACK], BF16, name="three_grouped", align_bytes=64)
+        three_codes = keep.tile([P, P], U32, name="three_codes", align_bytes=64)
+        three_scales = keep.tile([P, P], U8, name="three_scales", align_bytes=64)
+        parts = [slice(j * P // 2, (j + 1) * P // 2) for j in range(2)]
+        for part in parts:
+            wide = slice(part.start * PACK, part.stop * PACK)
+            lay(three_grouped[:, wide], turned_three[:, :, part])
+            quantize(three_codes[:, part], three_scales[:, part], three_grouped[:, wide])
+
+        y_two = bank("y_two", [NQ, P], 6)
+        product(y_two[:], two_codes[:], two_scales[:])
+        out_two = keep.tile([NQ, P], F32, name="out_two")
+        nc.scalar.activation(out_two[:], y_two[:], copy, scale=inverse[:])
+        nc.sync.dma_start(out[0, :, 2 * P : 3 * P], out_two[:])
+
+        out_three = keep.tile([NQ, P], F32, name="out_three")
         for j, part in enumerate(parts):
-            nc.tensor.matmul_mx(
-                out=y_last[j][:],
-                lhsT=w_codes[:].bitcast(FP8X4),
-                lhsT_scale=w_scales[:],
-                rhs=codes_3[:, part].bitcast(FP8X4),
-                rhs_scale=v_scales[:, 3, part],
-                start=True,
-                stop=True,
-            )
-            nc.vector.tensor_scalar(out_last[:, part], y_last[j][:], inverse[:], None, mult)
-        nc.sync.dma_start(out[0, :, 3 * P : DV], out_last[:])
+            y_three = bank(f"y_three{j}", [NQ, P // 2], (7, 4)[j])
+            product(y_three[:], three_codes[:, part], three_scales[:, part])
+            nc.vector.tensor_scalar(out_three[:, part], y_three[:], inverse[:], None, mult)
+        nc.sync.dma_start(out[0, :, 3 * P : DV], out_three[:])

@@ -55,14 +55,13 @@ def tile_attend_rbf_topk_kernel(tc, qT, kT, vT, vs, kb, offs, out):
             return offsets[:, first // PER_COLUMN : last // PER_COLUMN]
 
         k_rows = kT.rearrange("(m t) w -> m t w", t=PACK)
-        k_pair = keep.tile([P, 2, POOL], F32, name="k_pair")
-        k_two = keep.tile([P, POOL], F32, name="k_two")
-        k_three = reuse("k_three", [P, POOL], F32, 4 * WINDOW_BYTES)
+        k_pair = reuse("k_pair", [P, 2, POOL], F32, SPARE + 32 * SLOTS)
+        k_late = [reuse(f"k_late{t}", [P, POOL], F32, SPARE + (64 + 16 * t) * SLOTS) for t in range(2)]
         v_zero = reuse("v_zero", [P, POOL], F32, 0)
         v_one = reuse("v_one", [P, POOL], F32, WINDOW_BYTES)
         v_two = reuse("v_two", [P, POOL], F32, 2 * WINDOW_BYTES)
         v_three = reuse("v_three", [P, POOL], F32, 3 * WINDOW_BYTES)
-        q_raw = keep.tile([P, PACK, NQ], F32, name="q_raw")
+        q_raw = reuse("q_raw", [P, PACK, NQ], F32, SPARE - 2 * SLOTS)
         kb_win = keep.tile([P, POOL], F32, name="kb_win")
         vs_win = keep.tile([P, POOL], F32, name="vs_win")
         nc.sync.dma_start(q_raw[:], qT[0].rearrange("(m t) q -> m t q", t=PACK))
@@ -70,8 +69,8 @@ def tile_attend_rbf_topk_kernel(tc, qT, kT, vT, vs, kb, offs, out):
         nc.scalar.dma_start(kb_win[KB_ROW : KB_ROW + 1, :], kb[0:1, :])
         nc.scalar.dma_start(vs_win[VS_ROW : VS_ROW + 1, :], vs[0:1, :])
         nc.sync.dma_start(k_pair[:], k_rows[:, 0:2, :])
-        nc.sync.dma_start(k_two[:], k_rows[:, 2, :])
-        nc.sync.dma_start(k_three[:], k_rows[:, 3, :])
+        for t in range(2):
+            nc.sync.dma_start(k_late[t][:], k_rows[:, 2 + t, :])
         nc.sync.dma_start(v_zero[:], vT[0:P, :])
         nc.sync.dma_start(v_one[:], vT[P : 2 * P, :])
         nc.sync.dma_start(v_two[:], vT[2 * P : 3 * P, :])
@@ -97,12 +96,12 @@ def tile_attend_rbf_topk_kernel(tc, qT, kT, vT, vs, kb, offs, out):
         kb_turn = bank("kb_turn", [P, COLS, P], 0)
         for c in range(COLS):
             nc.tensor.transpose(kb_turn[:, c, :], kb_row[:, c * P : (c + 1) * P], ident[:])
-        kb_col = keep.tile([P, COLS], F32, name="kb_col")
+        kb_col = reuse("kb_col", [P, COLS], F32, SPARE + 2 * SLOTS)
         nc.scalar.copy(kb_col[:], kb_turn[:, :, KB_ROW])
         kb_spread = bank("kb_spread", [P, COLS, P], 1)
         for c in range(COLS):
             nc.tensor.transpose(kb_spread[:, c, :], kb_col[:, c : c + 1].to_broadcast([P, P]), ident[:])
-        kb_all = keep.tile([P, SLOTS], F32, name="kb_all")
+        kb_all = reuse("kb_all", [P, SLOTS], F32, SPARE + 24 * SLOTS)
         nc.scalar.copy(kb_all[:], kb_spread[:].rearrange("p c i -> p (c i)"))
 
         vs_turn = bank("vs_turn", [P, PACK, P], 2)
@@ -111,19 +110,22 @@ def tile_attend_rbf_topk_kernel(tc, qT, kT, vT, vs, kb, offs, out):
         vs_col = keep.tile([P, PACK], F32, name="vs_col")
         nc.scalar.copy(vs_col[:], vs_turn[:, :, VS_ROW])
 
-        k_grouped = keep.tile([P, SLOTS, PACK], BF16, name="k_grouped", align_bytes=64)
         k_first = keep.tile([P, 2, SLOTS], F32, name="k_first")
         for t in range(2):
             nc.vector.tensor_copy(k_first[:, t, :], k_pair[:, t, :].indirect(offsets[:]))
-        nc.scalar.copy(k_grouped[:, :, 0:2], k_first[:].rearrange("p t i -> p i t"))
-        nc.vector.tensor_copy(k_grouped[:, :, 2], k_two[:].indirect(offsets[:]))
+        k_grouped = reuse("k_grouped", [P, SLOTS, PACK], BF16, SPARE + 32 * SLOTS)
+        nc.vector.tensor_copy(k_grouped[:, :, 0:2], k_first[:].rearrange("p t i -> p i t"))
         halves = [slice(h * HALF, (h + 1) * HALF) for h in range(2)]
-        for h in range(2):
-            nc.vector.tensor_copy(k_grouped[:, halves[h], 3], k_three[:].indirect(listed(h * HALF, (h + 1) * HALF)))
+        k_upper = reuse("k_upper", [P, 2, HALF], F32, SPARE)
+        for t in range(2):
+            nc.vector.tensor_copy(k_grouped[:, halves[0], 2 + t], k_late[t][:].indirect(listed(0, HALF)))
+            nc.scalar.activation(k_upper[:, t, :], k_late[t][:].indirect(listed(HALF, SLOTS)), copy)
         k_codes = keep.tile([P, SLOTS], U32, name="k_codes", align_bytes=64)
         k_scales = keep.tile([P, SLOTS], U8, name="k_scales", align_bytes=64)
         score = [bank(f"score{h}", [NQ, HALF], 4 + h) for h in range(2)]
         for h in range(2):
+            if h == 1:
+                nc.vector.tensor_copy(k_grouped[:, halves[1], 2:4], k_upper[:].rearrange("p t i -> p i t"))
             nc.vector.quantize_mx(
                 out=k_codes[:, halves[h]].bitcast(FP8X4),
                 scales=k_scales[:, halves[h]],
@@ -145,19 +147,20 @@ def tile_attend_rbf_topk_kernel(tc, qT, kT, vT, vs, kb, offs, out):
         neg_m = keep.tile([NQ, 1], F32, name="neg_m")
         nc.vector.tensor_reduce(neg_m[:], neg[:], axis=mybir.AxisListType.X, op=minimum)
 
-        g_zero = reuse("g_zero", [P, SLOTS], BF16, 4 * WINDOW_BYTES)
+        g_zero = reuse("g_zero", [P, SLOTS], BF16, SPARE + 80 * SLOTS)
         nc.scalar.activation(g_zero[:], v_zero[:].indirect(offsets[:]), copy)
 
         p = reuse("p", [NQ, PACK, P], F32, 0)
-        total = keep.tile([NQ, 1], F32, name="total")
-        nc.scalar.activation(
-            p[:].rearrange("q t m -> q m t"),
-            neg[:].rearrange("q (m t) -> q m t", t=PACK),
-            exp,
-            bias=neg_m[:],
-            scale=-1.0,
-            accum_out=total[:],
-        )
+        sums = keep.tile([NQ, PAIRS], F32, name="sums")
+        for u in range(PAIRS):
+            nc.scalar.activation(
+                p[:, 2 * u : 2 * u + 2, :].rearrange("q t m -> q m t"),
+                neg[:].rearrange("q (m t) -> q m t", t=PACK)[:, :, 2 * u : 2 * u + 2],
+                exp,
+                bias=neg_m[:],
+                scale=-1.0,
+                accum_out=sums[:, u : u + 1],
+            )
         p_turn = bank("p_turn", [P, PACK, NQ], 6)
         for t in range(PACK):
             nc.tensor.transpose(p_turn[:, t, :], p[:, t, :], ident[:])
@@ -182,7 +185,7 @@ def tile_attend_rbf_topk_kernel(tc, qT, kT, vT, vs, kb, offs, out):
             nc.vector.tensor_copy(gathered[:, 0:SHARE], window[:].indirect(listed(0, SHARE)))
             nc.scalar.activation(gathered[:, SHARE:SLOTS], window[:].indirect(listed(SHARE, SLOTS)), copy)
 
-        g_one = keep.tile([P, SLOTS], BF16, name="g_one")
+        g_one = reuse("g_one", [P, SLOTS], BF16, SPARE + 26 * SLOTS)
         nc.vector.tensor_copy(g_one[:], v_one[:].indirect(offsets[:]))
         turned_zero = turn("turned_zero", in_order(g_zero), 5)
         turned_one = turn("turned_one", in_order(g_one), 1)
@@ -192,6 +195,8 @@ def tile_attend_rbf_topk_kernel(tc, qT, kT, vT, vs, kb, offs, out):
             w_grouped[:], p_turn[:].rearrange("p t q -> p q t"), vs_col[:].unsqueeze(1).to_broadcast([P, NQ, PACK]), mult
         )
         inverse = reuse("inverse", [NQ, 1], F32, WINDOW_BYTES + 2 * NQ * PACK)
+        total = reuse("total", [NQ, 1], F32, WINDOW_BYTES + 2 * NQ * PACK + 64)
+        nc.vector.tensor_tensor(total[:], sums[:, 0:1], sums[:, 1:2], mybir.AluOpType.add)
         nc.vector.reciprocal(inverse[:], total[:])
 
         pair_grouped = reuse("pair_grouped", [P, 2, P * PACK], BF16, SPARE + 2 * SLOTS)

@@ -19,8 +19,9 @@ DV = 512
 PACK = 4
 PAIRS = 2
 PER_COLUMN = 16
-KB_ROW = P - 1
-VS_ROW = P // 2 - 1
+PIECES = POOL // P
+KB_FIRST = P - PIECES
+VS_ROWS = (P // 2 - 1, P - 1)
 WINDOW_BYTES = 4 * POOL
 SPARE = 5 * WINDOW_BYTES
 HALF = SLOTS // 2
@@ -62,12 +63,14 @@ def tile_attend_rbf_topk_kernel(tc, qT, kT, vT, vs, kb, offs, out):
         v_two = reuse("v_two", [P, POOL], F32, 2 * WINDOW_BYTES)
         v_three = reuse("v_three", [P, POOL], F32, 3 * WINDOW_BYTES)
         q_raw = reuse("q_raw", [P, PACK, NQ], F32, SPARE - 2 * SLOTS)
-        kb_win = keep.tile([P, POOL], F32, name="kb_win")
-        vs_win = keep.tile([P, POOL], F32, name="vs_win")
+        kb_rows = keep.tile([P, P], F32, name="kb_rows")
+        vs_win = reuse("vs_win", [P, POOL], F32, SPARE + 96 * SLOTS)
         nc.sync.dma_start(q_raw[:], qT[0].rearrange("(m t) q -> m t q", t=PACK))
         nc.sync.dma_start(offsets[:], offs)
-        nc.scalar.dma_start(kb_win[KB_ROW : KB_ROW + 1, :], kb[0:1, :])
-        nc.scalar.dma_start(vs_win[VS_ROW : VS_ROW + 1, :], vs[0:1, :])
+        nc.sync.dma_start(kb_rows[KB_FIRST:P, :], kb[0, :].rearrange("(r j) -> r j", j=P))
+        for h, row in enumerate(VS_ROWS):
+            tokens = slice(h * POOL // 2, (h + 1) * POOL // 2)
+            nc.sync.dma_start(vs_win[row : row + 1, tokens], vs[0:1, tokens])
         nc.sync.dma_start(k_pair[:], k_rows[:, 0:2, :])
         for t in range(2):
             nc.sync.dma_start(k_late[t][:], k_rows[:, 2 + t, :])
@@ -78,14 +81,10 @@ def tile_attend_rbf_topk_kernel(tc, qT, kT, vT, vs, kb, offs, out):
 
         ident = keep.tile([P, P], F32, name="ident")
         make_identity(nc, ident[:])
-        nc.vector.memset(kb_win[0:KB_ROW, :], 0.0)
-        nc.vector.memset(vs_win[0:VS_ROW, :], 0.0)
-        nc.gpsimd.memset(vs_win[VS_ROW + 1 : P, :], 0.0)
-
-        kb_row = keep.tile([P, SLOTS], F32, name="kb_row")
-        nc.vector.tensor_copy(kb_row[:], kb_win[:].indirect(offsets[:]))
-        vs_row = keep.tile([P, SLOTS], F32, name="vs_row")
-        nc.vector.tensor_copy(vs_row[:], vs_win[:].indirect(offsets[:]))
+        nc.vector.memset(kb_rows[0:KB_FIRST, :], 0.0)
+        nc.vector.memset(vs_win[0 : VS_ROWS[0], 0 : POOL // 2], 0.0)
+        nc.vector.memset(vs_win[0 : VS_ROWS[1], POOL // 2 : POOL], 0.0)
+        nc.gpsimd.memset(vs_win[VS_ROWS[0] + 1 : P, 0 : POOL // 2], 0.0)
 
         q_grouped = keep.tile([P, NQ, PACK], BF16, name="q_grouped", align_bytes=64)
         q_codes = keep.tile([P, NQ], U32, name="q_codes", align_bytes=64)
@@ -93,22 +92,27 @@ def tile_attend_rbf_topk_kernel(tc, qT, kT, vT, vs, kb, offs, out):
         nc.scalar.copy(q_grouped[:], q_raw[:].rearrange("p t q -> p q t"))
         nc.vector.quantize_mx(out=q_codes[:].bitcast(FP8X4), scales=q_scales[:], in_=q_grouped[:].rearrange("p q t -> p (q t)"))
 
-        kb_turn = bank("kb_turn", [P, COLS, P], 0)
-        for c in range(COLS):
-            nc.tensor.transpose(kb_turn[:, c, :], kb_row[:, c * P : (c + 1) * P], ident[:])
-        kb_col = reuse("kb_col", [P, COLS], F32, SPARE + 2 * SLOTS)
-        nc.scalar.copy(kb_col[:], kb_turn[:, :, KB_ROW])
-        kb_spread = bank("kb_spread", [P, COLS, P], 1)
-        for c in range(COLS):
-            nc.tensor.transpose(kb_spread[:, c, :], kb_col[:, c : c + 1].to_broadcast([P, P]), ident[:])
-        kb_all = reuse("kb_all", [P, SLOTS], F32, SPARE + 24 * SLOTS)
-        nc.scalar.copy(kb_all[:], kb_spread[:].rearrange("p c i -> p (c i)"))
+        vs_row = reuse("vs_row", [P, SLOTS], F32, SPARE - 4 * SLOTS)
+        nc.scalar.activation(vs_row[:], vs_win[:].indirect(offsets[:]), copy)
 
-        vs_turn = bank("vs_turn", [P, PACK, P], 2)
+        kb_turn = bank("kb_turn", [P, P], 4)
+        nc.tensor.transpose(kb_turn[:], kb_rows[:], ident[:])
+        kb_col = keep.tile([P, PIECES], F32, name="kb_col")
+        nc.vector.tensor_copy(kb_col[:], kb_turn[:, KB_FIRST:P])
+        kb_win = reuse("kb_win", [P, POOL], F32, SPARE + 112 * SLOTS)
+        for b in range(PIECES // COLS):
+            spread = bank(f"kb_spread{b}", [P, COLS, P], b)
+            for c in range(COLS):
+                r = b * COLS + c
+                nc.tensor.transpose(spread[:, c, :], kb_col[:, r : r + 1].to_broadcast([P, P]), ident[:])
+            move = nc.vector.tensor_copy if b < 2 else nc.scalar.copy
+            move(kb_win[:, b * SLOTS : (b + 1) * SLOTS], spread[:].rearrange("p c j -> p (c j)"))
+        kb_all = reuse("kb_all", [P, SLOTS], F32, SPARE + 24 * SLOTS)
+        nc.scalar.activation(kb_all[:], kb_win[:].indirect(offsets[:]), copy)
+
+        vs_turn = bank("vs_turn", [P, PACK, P], 3)
         for t in range(PACK):
             nc.tensor.transpose(vs_turn[:, t, :], vs_row[:, t:SLOTS:PACK], ident[:])
-        vs_col = keep.tile([P, PACK], F32, name="vs_col")
-        nc.scalar.copy(vs_col[:], vs_turn[:, :, VS_ROW])
 
         k_first = keep.tile([P, 2, SLOTS], F32, name="k_first")
         for t in range(2):
@@ -116,16 +120,15 @@ def tile_attend_rbf_topk_kernel(tc, qT, kT, vT, vs, kb, offs, out):
         k_grouped = reuse("k_grouped", [P, SLOTS, PACK], BF16, SPARE + 32 * SLOTS)
         nc.vector.tensor_copy(k_grouped[:, :, 0:2], k_first[:].rearrange("p t i -> p i t"))
         halves = [slice(h * HALF, (h + 1) * HALF) for h in range(2)]
-        k_upper = reuse("k_upper", [P, 2, HALF], F32, SPARE)
+        k_upper = reuse("k_upper", [P, 2, HALF], F32, SPARE + 112 * SLOTS)
         for t in range(2):
             nc.vector.tensor_copy(k_grouped[:, halves[0], 2 + t], k_late[t][:].indirect(listed(0, HALF)))
             nc.scalar.activation(k_upper[:, t, :], k_late[t][:].indirect(listed(HALF, SLOTS)), copy)
-        k_codes = keep.tile([P, SLOTS], U32, name="k_codes", align_bytes=64)
+        nc.vector.tensor_copy(k_grouped[:, halves[1], 2:4], k_upper[:].rearrange("p t i -> p i t"))
+        k_codes = reuse("k_codes", [P, SLOTS], U32, SPARE + 112 * SLOTS)
         k_scales = keep.tile([P, SLOTS], U8, name="k_scales", align_bytes=64)
         score = [bank(f"score{h}", [NQ, HALF], 4 + h) for h in range(2)]
         for h in range(2):
-            if h == 1:
-                nc.vector.tensor_copy(k_grouped[:, halves[1], 2:4], k_upper[:].rearrange("p t i -> p i t"))
             nc.vector.quantize_mx(
                 out=k_codes[:, halves[h]].bitcast(FP8X4),
                 scales=k_scales[:, halves[h]],
@@ -141,11 +144,14 @@ def tile_attend_rbf_topk_kernel(tc, qT, kT, vT, vs, kb, offs, out):
                 stop=True,
             )
 
-        neg = reuse("neg", [NQ, SLOTS], F32, SPARE)
+        neg = reuse("neg", [NQ, SLOTS], F32, SPARE + 36 * SLOTS)
         for h in range(2):
             nc.vector.scalar_tensor_tensor(neg[:, halves[h]], score[h][:], -1.0, kb_all[:, halves[h]], mult, subtract)
         neg_m = keep.tile([NQ, 1], F32, name="neg_m")
         nc.vector.tensor_reduce(neg_m[:], neg[:], axis=mybir.AxisListType.X, op=minimum)
+
+        vs_col = reuse("vs_col", [P, PACK], F32, SPARE + 24 * SLOTS)
+        nc.vector.tensor_reduce(vs_col[:], vs_turn[:, :, VS_ROWS[0] : P : P // 2], axis=mybir.AxisListType.X, op=mybir.AluOpType.add)
 
         g_zero = reuse("g_zero", [P, SLOTS], BF16, SPARE + 80 * SLOTS)
         nc.scalar.activation(g_zero[:], v_zero[:].indirect(offsets[:]), copy)
@@ -161,6 +167,8 @@ def tile_attend_rbf_topk_kernel(tc, qT, kT, vT, vs, kb, offs, out):
                 scale=-1.0,
                 accum_out=sums[:, u : u + 1],
             )
+        total = keep.tile([NQ, 1], F32, name="total")
+        nc.scalar.activation(total[:], sums[:, 0:1], mybir.ActivationFunctionType.Identity, bias=sums[:, 1:2])
         p_turn = bank("p_turn", [P, PACK, NQ], 6)
         for t in range(PACK):
             nc.tensor.transpose(p_turn[:, t, :], p[:, t, :], ident[:])
@@ -195,15 +203,13 @@ def tile_attend_rbf_topk_kernel(tc, qT, kT, vT, vs, kb, offs, out):
             w_grouped[:], p_turn[:].rearrange("p t q -> p q t"), vs_col[:].unsqueeze(1).to_broadcast([P, NQ, PACK]), mult
         )
         inverse = reuse("inverse", [NQ, 1], F32, WINDOW_BYTES + 2 * NQ * PACK)
-        total = reuse("total", [NQ, 1], F32, WINDOW_BYTES + 2 * NQ * PACK + 64)
-        nc.vector.tensor_tensor(total[:], sums[:, 0:1], sums[:, 1:2], mybir.AluOpType.add)
         nc.vector.reciprocal(inverse[:], total[:])
 
-        pair_grouped = reuse("pair_grouped", [P, 2, P * PACK], BF16, SPARE + 2 * SLOTS)
+        pair_grouped = reuse("pair_grouped", [P, 2, P * PACK], BF16, SPARE + 38 * SLOTS)
         lay(pair_grouped[:, 0, :], turned_zero[:])
         lay(pair_grouped[:, 1, :], turned_one[:], nc.vector.tensor_copy)
 
-        g_two = reuse("g_two", [P, SLOTS], BF16, SPARE)
+        g_two = reuse("g_two", [P, SLOTS], BF16, SPARE + 36 * SLOTS)
         nc.scalar.activation(g_two[:], v_two[:].indirect(offsets[:]), copy)
         turned_two = turn("turned_two", in_order(g_two), 2)
 
@@ -228,7 +234,7 @@ def tile_attend_rbf_topk_kernel(tc, qT, kT, vT, vs, kb, offs, out):
         y_pair = bank("y_pair", [NQ, 2 * P], 0)
         product(y_pair[:], pair_codes[:], pair_scales[:])
 
-        g_three = reuse("g_three", [P, SLOTS], BF16, SPARE + 4 * SLOTS)
+        g_three = reuse("g_three", [P, SLOTS], BF16, SPARE + 40 * SLOTS)
         gather_shared(g_three, v_three)
         turned_three = turn("turned_three", in_order(g_three), 3)
 

@@ -21,13 +21,12 @@ PAIRS = 2
 PER_COLUMN = 16
 PIECES = POOL // P
 KB_FIRST = P - PIECES
-VS_ROWS = (P // 2 - 1, P - 1)
-WINDOW_BYTES = 4 * POOL
-SPARE = 5 * WINDOW_BYTES
+QUARTERS = 2
+VS_ROWS = slice(63, 128, 64)
 HALF = SLOTS // 2
-SHARE = 256
 BANK = 2048
 COLS = SLOTS // P
+KIB = 1024
 
 FLOPS = 2 * NQ * SLOTS * (D + DV)
 BYTES = 4 * ((D + DV) * POOL + 2 * POOL + D * NQ + NQ * DV) + 2 * P * (SLOTS // PER_COLUMN)
@@ -37,6 +36,7 @@ def tile_attend_rbf_topk_kernel(tc, qT, kT, vT, vs, kb, offs, out):
     nc = tc.nc
     exp = mybir.ActivationFunctionType.Exp
     copy = mybir.ActivationFunctionType.Copy
+    identity = mybir.ActivationFunctionType.Identity
     mult, subtract, minimum = mybir.AluOpType.mult, mybir.AluOpType.subtract, mybir.AluOpType.min
 
     with ExitStack() as ctx:
@@ -44,36 +44,60 @@ def tile_attend_rbf_topk_kernel(tc, qT, kT, vT, vs, kb, offs, out):
         over = ctx.enter_context(tc.tile_pool(name="over", bufs=1))
         psum = ctx.enter_context(tc.psum_pool(name="psum", bufs=1))
 
-        def reuse(name, shape, dtype, offset):
+        def placed(name, shape, dtype, offset):
             return over.tile(shape, dtype, name=name, offset=offset, align_bytes=64)
 
         def bank(name, shape, number):
             return psum.tile(shape, F32, name=name, offset=number * BANK)
 
+        def plane(window, t):
+            return window[:, t * POOL : (t + 1) * POOL]
+
+        def quantize(codes, scales, grouped):
+            nc.vector.quantize_mx(out=codes.bitcast(FP8X4), scales=scales, in_=grouped)
+
+        def product(y, lhs_codes, lhs_scales, codes, scales):
+            nc.tensor.matmul_mx(
+                out=y,
+                lhsT=lhs_codes.bitcast(FP8X4),
+                lhsT_scale=lhs_scales,
+                rhs=codes.bitcast(FP8X4),
+                rhs_scale=scales,
+                start=True,
+                stop=True,
+            )
+
         offsets = keep.tile([P, SLOTS // PER_COLUMN], U16, name="offsets")
+        halves = [slice(h * HALF, (h + 1) * HALF) for h in range(2)]
 
-        def listed(first, last):
-            return offsets[:, first // PER_COLUMN : last // PER_COLUMN]
+        def listed(slots):
+            return offsets[:, slots.start // PER_COLUMN : slots.stop // PER_COLUMN]
 
-        k_rows = kT.rearrange("(m t) w -> m t w", t=PACK)
-        k_pair = reuse("k_pair", [P, 2, POOL], F32, SPARE + 32 * SLOTS)
-        k_late = [reuse(f"k_late{t}", [P, POOL], F32, SPARE + (64 + 16 * t) * SLOTS) for t in range(2)]
-        v_zero = reuse("v_zero", [P, POOL], F32, 0)
-        v_one = reuse("v_one", [P, POOL], F32, WINDOW_BYTES)
-        v_two = reuse("v_two", [P, POOL], F32, 2 * WINDOW_BYTES)
-        v_three = reuse("v_three", [P, POOL], F32, 3 * WINDOW_BYTES)
-        q_raw = reuse("q_raw", [P, PACK, NQ], F32, SPARE - 2 * SLOTS)
+        K_EARLY, K_TWO, K_THREE, V_ZERO, V_ONE, V_TWO, V_THREE = (KIB * at for at in (0, 16, 24, 32, 40, 48, 56))
+        KB_ALL, NEG, Q_RAW, KB_WIN, VS_WIN = 64 * KIB, 66 * KIB, 68 * KIB, 72 * KIB, 80 * KIB
+        k_rows = kT.rearrange("(m t) w -> m (t w)", t=PACK)
+        k_early = placed("k_early", [P, 2 * POOL], F32, K_EARLY)
+        k_late = [placed(f"k_late{t}", [P, POOL], F32, place) for t, place in enumerate((K_TWO, K_THREE))]
+        v_zero = placed("v_zero", [P, POOL], F32, V_ZERO)
+        v_one = placed("v_one", [P, POOL], F32, V_ONE)
+        v_two = placed("v_two", [P, POOL], F32, V_TWO)
+        v_three = placed("v_three", [P, POOL], F32, V_THREE)
         kb_rows = keep.tile([P, P], F32, name="kb_rows")
-        vs_win = reuse("vs_win", [P, POOL], F32, SPARE + 96 * SLOTS)
-        nc.sync.dma_start(q_raw[:], qT[0].rearrange("(m t) q -> m t q", t=PACK))
+        vs_win = placed("vs_win", [P, POOL], F32, VS_WIN)
+        q_raw = placed("q_raw", [P, PACK, NQ], F32, Q_RAW)
+        nc.sync.dma_start(k_early[:], k_rows[:, 0 : 2 * POOL])
         nc.sync.dma_start(offsets[:], offs)
-        nc.sync.dma_start(kb_rows[KB_FIRST:P, :], kb[0, :].rearrange("(r j) -> r j", j=P))
-        for h, row in enumerate(VS_ROWS):
-            tokens = slice(h * POOL // 2, (h + 1) * POOL // 2)
+        nc.vector.memset(kb_rows[0:KB_FIRST, :], 0.0)
+        nc.vector.memset(vs_win[0:63, 0 : POOL // 2], 0.0)
+        nc.vector.memset(vs_win[64:P, 0 : POOL // 2], 0.0)
+        nc.vector.memset(vs_win[0:127, POOL // 2 : POOL], 0.0)
+        nc.scalar.dma_start(kb_rows[KB_FIRST:P, :], kb[0, :].rearrange("(r j) -> r j", j=P))
+        for quarter, row in enumerate(range(P)[VS_ROWS]):
+            tokens = slice(quarter * POOL // QUARTERS, (quarter + 1) * POOL // QUARTERS)
             nc.sync.dma_start(vs_win[row : row + 1, tokens], vs[0:1, tokens])
-        nc.sync.dma_start(k_pair[:], k_rows[:, 0:2, :])
         for t in range(2):
-            nc.sync.dma_start(k_late[t][:], k_rows[:, 2 + t, :])
+            nc.sync.dma_start(k_late[t][:], k_rows[:, (2 + t) * POOL : (3 + t) * POOL])
+        nc.sync.dma_start(q_raw[:], qT[0].rearrange("(m t) q -> m t q", t=PACK))
         nc.sync.dma_start(v_zero[:], vT[0:P, :])
         nc.sync.dma_start(v_one[:], vT[P : 2 * P, :])
         nc.sync.dma_start(v_two[:], vT[2 * P : 3 * P, :])
@@ -81,82 +105,63 @@ def tile_attend_rbf_topk_kernel(tc, qT, kT, vT, vs, kb, offs, out):
 
         ident = keep.tile([P, P], F32, name="ident")
         make_identity(nc, ident[:])
-        nc.vector.memset(kb_rows[0:KB_FIRST, :], 0.0)
-        nc.vector.memset(vs_win[0 : VS_ROWS[0], 0 : POOL // 2], 0.0)
-        nc.vector.memset(vs_win[0 : VS_ROWS[1], POOL // 2 : POOL], 0.0)
-        nc.gpsimd.memset(vs_win[VS_ROWS[0] + 1 : P, 0 : POOL // 2], 0.0)
-
-        q_grouped = keep.tile([P, NQ, PACK], BF16, name="q_grouped", align_bytes=64)
-        q_codes = keep.tile([P, NQ], U32, name="q_codes", align_bytes=64)
-        q_scales = keep.tile([P, NQ], U8, name="q_scales", align_bytes=64)
-        nc.scalar.copy(q_grouped[:], q_raw[:].rearrange("p t q -> p q t"))
-        nc.vector.quantize_mx(out=q_codes[:].bitcast(FP8X4), scales=q_scales[:], in_=q_grouped[:].rearrange("p q t -> p (q t)"))
-
-        vs_row = reuse("vs_row", [P, SLOTS], F32, SPARE - 4 * SLOTS)
-        nc.scalar.activation(vs_row[:], vs_win[:].indirect(offsets[:]), copy)
 
         kb_turn = bank("kb_turn", [P, P], 4)
         nc.tensor.transpose(kb_turn[:], kb_rows[:], ident[:])
         kb_col = keep.tile([P, PIECES], F32, name="kb_col")
-        nc.vector.tensor_copy(kb_col[:], kb_turn[:, KB_FIRST:P])
-        kb_win = reuse("kb_win", [P, POOL], F32, SPARE + 112 * SLOTS)
+        nc.scalar.copy(kb_col[:], kb_turn[:, KB_FIRST:P])
+        kb_win = placed("kb_win", [P, POOL], F32, KB_WIN)
         for b in range(PIECES // COLS):
-            spread = bank(f"kb_spread{b}", [P, COLS, P], b)
+            spread = bank(f"kb_spread{b}", [P, COLS, P], (0, 1, 3, 5)[b])
             for c in range(COLS):
                 r = b * COLS + c
                 nc.tensor.transpose(spread[:, c, :], kb_col[:, r : r + 1].to_broadcast([P, P]), ident[:])
-            move = nc.vector.tensor_copy if b < 2 else nc.scalar.copy
-            move(kb_win[:, b * SLOTS : (b + 1) * SLOTS], spread[:].rearrange("p c j -> p (c j)"))
-        kb_all = reuse("kb_all", [P, SLOTS], F32, SPARE + 24 * SLOTS)
+            nc.scalar.copy(kb_win[:, b * SLOTS : (b + 1) * SLOTS], spread[:].rearrange("p c j -> p (c j)"))
+        kb_all = placed("kb_all", [P, SLOTS], F32, KB_ALL)
         nc.scalar.activation(kb_all[:], kb_win[:].indirect(offsets[:]), copy)
-
-        vs_turn = bank("vs_turn", [P, PACK, P], 3)
+        vs_row = placed("vs_row", [P, SLOTS], F32, KB_WIN)
+        nc.scalar.activation(vs_row[:], vs_win[:].indirect(offsets[:]), copy)
+        vs_turn = bank("vs_turn", [P, PACK, P], 2)
         for t in range(PACK):
             nc.tensor.transpose(vs_turn[:, t, :], vs_row[:, t:SLOTS:PACK], ident[:])
 
-        k_first = keep.tile([P, 2, SLOTS], F32, name="k_first")
+        planes = keep.tile([P, 2, SLOTS], F32, name="planes")
         for t in range(2):
-            nc.vector.tensor_copy(k_first[:, t, :], k_pair[:, t, :].indirect(offsets[:]))
-        k_grouped = reuse("k_grouped", [P, SLOTS, PACK], BF16, SPARE + 32 * SLOTS)
-        nc.vector.tensor_copy(k_grouped[:, :, 0:2], k_first[:].rearrange("p t i -> p i t"))
-        halves = [slice(h * HALF, (h + 1) * HALF) for h in range(2)]
-        k_upper = reuse("k_upper", [P, 2, HALF], F32, SPARE + 112 * SLOTS)
+            nc.vector.tensor_copy(planes[:, t, :], plane(k_early, t).indirect(offsets[:]))
+        k_grouped = placed("k_grouped", [P, SLOTS, PACK], BF16, K_EARLY)
+        nc.vector.tensor_copy(k_grouped[:, :, 0:2], planes[:].rearrange("p t i -> p i t"))
+
+        upper = placed("upper", [P, 2, HALF], F32, VS_WIN)
         for t in range(2):
-            nc.vector.tensor_copy(k_grouped[:, halves[0], 2 + t], k_late[t][:].indirect(listed(0, HALF)))
-            nc.scalar.activation(k_upper[:, t, :], k_late[t][:].indirect(listed(HALF, SLOTS)), copy)
-        nc.vector.tensor_copy(k_grouped[:, halves[1], 2:4], k_upper[:].rearrange("p t i -> p i t"))
-        k_codes = reuse("k_codes", [P, SLOTS], U32, SPARE + 112 * SLOTS)
+            nc.vector.tensor_copy(k_grouped[:, halves[0], 2 + t], k_late[t][:].indirect(listed(halves[0])))
+            nc.scalar.activation(upper[:, t, :], k_late[t][:].indirect(listed(halves[1])), copy)
+        q_grouped = placed("q_grouped", [P, NQ, PACK], BF16, K_THREE)
+        nc.scalar.copy(q_grouped[:], q_raw[:].rearrange("p t q -> p q t"))
+        nc.vector.tensor_copy(k_grouped[:, halves[1], 2:4], upper[:].rearrange("p t i -> p i t"))
+
+        k_codes = placed("k_codes", [P, SLOTS], U32, VS_WIN)
         k_scales = keep.tile([P, SLOTS], U8, name="k_scales", align_bytes=64)
-        score = [bank(f"score{h}", [NQ, HALF], 4 + h) for h in range(2)]
-        for h in range(2):
-            nc.vector.quantize_mx(
-                out=k_codes[:, halves[h]].bitcast(FP8X4),
-                scales=k_scales[:, halves[h]],
-                in_=k_grouped[:, halves[h], :].rearrange("p i t -> p (i t)"),
-            )
-            nc.tensor.matmul_mx(
-                out=score[h][:],
-                lhsT=q_codes[:].bitcast(FP8X4),
-                lhsT_scale=q_scales[:],
-                rhs=k_codes[:, halves[h]].bitcast(FP8X4),
-                rhs_scale=k_scales[:, halves[h]],
-                start=True,
-                stop=True,
-            )
+        q_codes = keep.tile([P, NQ], U32, name="q_codes", align_bytes=64)
+        q_scales = keep.tile([P, NQ], U8, name="q_scales", align_bytes=64)
+        score = [bank(f"score{h}", [NQ, HALF], 3 + h) for h in range(2)]
+        for h, half in enumerate(halves):
+            quantize(k_codes[:, half], k_scales[:, half], k_grouped[:, half, :].rearrange("p i t -> p (i t)"))
+            if h == 0:
+                quantize(q_codes[:], q_scales[:], q_grouped[:].rearrange("p q t -> p (q t)"))
+            product(score[h][:], q_codes[:], q_scales[:], k_codes[:, half], k_scales[:, half])
 
-        neg = reuse("neg", [NQ, SLOTS], F32, SPARE + 36 * SLOTS)
-        for h in range(2):
-            nc.vector.scalar_tensor_tensor(neg[:, halves[h]], score[h][:], -1.0, kb_all[:, halves[h]], mult, subtract)
-        neg_m = keep.tile([NQ, 1], F32, name="neg_m")
-        nc.vector.tensor_reduce(neg_m[:], neg[:], axis=mybir.AxisListType.X, op=minimum)
-
-        vs_col = reuse("vs_col", [P, PACK], F32, SPARE + 24 * SLOTS)
-        nc.vector.tensor_reduce(vs_col[:], vs_turn[:, :, VS_ROWS[0] : P : P // 2], axis=mybir.AxisListType.X, op=mybir.AluOpType.add)
-
-        g_zero = reuse("g_zero", [P, SLOTS], BF16, SPARE + 80 * SLOTS)
+        g_zero = placed("g_zero", [P, SLOTS], BF16, Q_RAW)
         nc.scalar.activation(g_zero[:], v_zero[:].indirect(offsets[:]), copy)
 
-        p = reuse("p", [NQ, PACK, P], F32, 0)
+        neg = placed("neg", [NQ, SLOTS], F32, NEG)
+        for h, half in enumerate(halves):
+            nc.vector.scalar_tensor_tensor(neg[:, half], score[h][:], -1.0, kb_all[:, half], mult, subtract)
+        neg_m = keep.tile([NQ, 1], F32, name="neg_m")
+        nc.vector.tensor_reduce(neg_m[:], neg[:], axis=mybir.AxisListType.X, op=minimum)
+        vs_col = placed("vs_col", [P, PACK], F32, KB_ALL + KIB)
+        nc.vector.tensor_reduce(vs_col[:], vs_turn[:, :, VS_ROWS], axis=mybir.AxisListType.X, op=mybir.AluOpType.add)
+
+        p = placed("p", [NQ, PACK, P], F32, V_ZERO)
         sums = keep.tile([NQ, PAIRS], F32, name="sums")
         for u in range(PAIRS):
             nc.scalar.activation(
@@ -167,9 +172,7 @@ def tile_attend_rbf_topk_kernel(tc, qT, kT, vT, vs, kb, offs, out):
                 scale=-1.0,
                 accum_out=sums[:, u : u + 1],
             )
-        total = keep.tile([NQ, 1], F32, name="total")
-        nc.scalar.activation(total[:], sums[:, 0:1], mybir.ActivationFunctionType.Identity, bias=sums[:, 1:2])
-        p_turn = bank("p_turn", [P, PACK, NQ], 6)
+        p_turn = bank("p_turn", [P, PACK, NQ], 5)
         for t in range(PACK):
             nc.tensor.transpose(p_turn[:, t, :], p[:, t, :], ident[:])
 
@@ -183,69 +186,51 @@ def tile_attend_rbf_topk_kernel(tc, qT, kT, vT, vs, kb, offs, out):
             words = gathered[:].bitcast(F32)
             return lambda u: words[:, u : SLOTS // 2 : PAIRS]
 
-        def lay(grouped, turned, move=nc.scalar.copy):
+        def lay(grouped, turned, move):
             move(grouped.bitcast(F32).rearrange("p (e u) -> p e u", u=PAIRS), turned.rearrange("p u e -> p e u"))
 
-        def quantize(codes, scales, grouped):
-            nc.vector.quantize_mx(out=codes.bitcast(FP8X4), scales=scales, in_=grouped)
-
-        def gather_shared(gathered, window):
-            nc.vector.tensor_copy(gathered[:, 0:SHARE], window[:].indirect(listed(0, SHARE)))
-            nc.scalar.activation(gathered[:, SHARE:SLOTS], window[:].indirect(listed(SHARE, SLOTS)), copy)
-
-        g_one = reuse("g_one", [P, SLOTS], BF16, SPARE + 26 * SLOTS)
+        g_one = placed("g_one", [P, SLOTS], BF16, KB_ALL)
         nc.vector.tensor_copy(g_one[:], v_one[:].indirect(offsets[:]))
-        turned_zero = turn("turned_zero", in_order(g_zero), 5)
-        turned_one = turn("turned_one", in_order(g_one), 1)
+        total = keep.tile([NQ, 1], F32, name="total")
+        nc.scalar.activation(total[:], sums[:, 0:1], identity, bias=sums[:, 1:2])
+        turned_zero = turn("turned_zero", in_order(g_zero), 4)
+        pair_grouped = placed("pair_grouped", [P, 2, P * PACK], BF16, NEG + 64)
+        lay(pair_grouped[:, 0, :], turned_zero[:], nc.scalar.copy)
+        turned_one = turn("turned_one", in_order(g_one), 4)
 
-        w_grouped = reuse("w_grouped", [P, NQ, PACK], BF16, WINDOW_BYTES)
+        w_grouped = keep.tile([P, NQ, PACK], BF16, name="w_grouped", align_bytes=64)
         nc.vector.tensor_tensor(
             w_grouped[:], p_turn[:].rearrange("p t q -> p q t"), vs_col[:].unsqueeze(1).to_broadcast([P, NQ, PACK]), mult
         )
-        inverse = reuse("inverse", [NQ, 1], F32, WINDOW_BYTES + 2 * NQ * PACK)
-        nc.vector.reciprocal(inverse[:], total[:])
-
-        pair_grouped = reuse("pair_grouped", [P, 2, P * PACK], BF16, SPARE + 38 * SLOTS)
-        lay(pair_grouped[:, 0, :], turned_zero[:])
         lay(pair_grouped[:, 1, :], turned_one[:], nc.vector.tensor_copy)
-
-        g_two = reuse("g_two", [P, SLOTS], BF16, SPARE + 36 * SLOTS)
-        nc.scalar.activation(g_two[:], v_two[:].indirect(offsets[:]), copy)
-        turned_two = turn("turned_two", in_order(g_two), 2)
-
         w_codes = keep.tile([P, NQ], U32, name="w_codes", align_bytes=64)
         w_scales = keep.tile([P, NQ], U8, name="w_scales", align_bytes=64)
         quantize(w_codes[:], w_scales[:], w_grouped[:].rearrange("p q t -> p (q t)"))
+        inverse = placed("inverse", [NQ, 1], F32, V_ONE)
+        nc.vector.reciprocal(inverse[:], total[:])
         pair_codes = keep.tile([P, 2 * P], U32, name="pair_codes", align_bytes=64)
         pair_scales = keep.tile([P, 2 * P], U8, name="pair_scales", align_bytes=64)
         quantize(pair_codes[:], pair_scales[:], pair_grouped[:].rearrange("p b x -> p (b x)"))
+        y_pair = bank("y_pair", [NQ, 2 * P], 6)
+        product(y_pair[:], w_codes[:], w_scales[:], pair_codes[:], pair_scales[:])
 
-        def product(y, codes, scales):
-            nc.tensor.matmul_mx(
-                out=y,
-                lhsT=w_codes[:].bitcast(FP8X4),
-                lhsT_scale=w_scales[:],
-                rhs=codes.bitcast(FP8X4),
-                rhs_scale=scales,
-                start=True,
-                stop=True,
-            )
+        g_two = placed("g_two", [P, SLOTS], BF16, V_ONE + KIB)
+        nc.scalar.activation(g_two[:], v_two[:].indirect(offsets[:]), copy)
+        turned_two = turn("turned_two", in_order(g_two), 1)
 
-        y_pair = bank("y_pair", [NQ, 2 * P], 0)
-        product(y_pair[:], pair_codes[:], pair_scales[:])
-
-        g_three = reuse("g_three", [P, SLOTS], BF16, SPARE + 40 * SLOTS)
-        gather_shared(g_three, v_three)
+        g_three = placed("g_three", [P, SLOTS], BF16, NEG + KIB)
+        nc.vector.tensor_copy(g_three[:, halves[0]], v_three[:].indirect(listed(halves[0])))
+        nc.scalar.activation(g_three[:, halves[1]], v_three[:].indirect(listed(halves[1])), copy)
         turned_three = turn("turned_three", in_order(g_three), 3)
 
-        two_grouped = reuse("two_grouped", [P, P * PACK], BF16, 3 * WINDOW_BYTES)
-        lay(two_grouped[:], turned_two[:])
-        two_codes = keep.tile([P, P], U32, name="two_codes", align_bytes=64)
-        two_scales = keep.tile([P, P], U8, name="two_scales", align_bytes=64)
-        out_pair = reuse("out_pair", [NQ, 2 * P], F32, 3 * WINDOW_BYTES + 2 * P * PACK)
+        two_grouped = placed("two_grouped", [P, P * PACK], BF16, V_THREE)
+        lay(two_grouped[:], turned_two[:], nc.scalar.copy)
+        out_pair = placed("out_pair", [NQ, 2 * P], F32, V_THREE + KIB)
         nc.vector.tensor_scalar(out_pair[:], y_pair[:], inverse[:], None, mult)
         nc.sync.dma_start(out[0, :, 0 : 2 * P], out_pair[:])
 
+        two_codes = keep.tile([P, P], U32, name="two_codes", align_bytes=64)
+        two_scales = keep.tile([P, P], U8, name="two_scales", align_bytes=64)
         quantize(two_codes[:], two_scales[:], two_grouped[:])
         three_grouped = keep.tile([P, P * PACK], BF16, name="three_grouped", align_bytes=64)
         three_codes = keep.tile([P, P], U32, name="three_codes", align_bytes=64)
@@ -253,11 +238,11 @@ def tile_attend_rbf_topk_kernel(tc, qT, kT, vT, vs, kb, offs, out):
         parts = [slice(j * P // 2, (j + 1) * P // 2) for j in range(2)]
         for part in parts:
             wide = slice(part.start * PACK, part.stop * PACK)
-            lay(three_grouped[:, wide], turned_three[:, :, part])
+            lay(three_grouped[:, wide], turned_three[:, :, part], nc.scalar.copy)
             quantize(three_codes[:, part], three_scales[:, part], three_grouped[:, wide])
 
-        y_two = bank("y_two", [NQ, P], 6)
-        product(y_two[:], two_codes[:], two_scales[:])
+        y_two = bank("y_two", [NQ, P], 5)
+        product(y_two[:], w_codes[:], w_scales[:], two_codes[:], two_scales[:])
         out_two = keep.tile([NQ, P], F32, name="out_two")
         nc.scalar.activation(out_two[:], y_two[:], copy, scale=inverse[:])
         nc.sync.dma_start(out[0, :, 2 * P : 3 * P], out_two[:])
@@ -265,6 +250,6 @@ def tile_attend_rbf_topk_kernel(tc, qT, kT, vT, vs, kb, offs, out):
         out_three = keep.tile([NQ, P], F32, name="out_three")
         for j, part in enumerate(parts):
             y_three = bank(f"y_three{j}", [NQ, P // 2], (7, 4)[j])
-            product(y_three[:], three_codes[:, part], three_scales[:, part])
+            product(y_three[:], w_codes[:], w_scales[:], three_codes[:, part], three_scales[:, part])
             nc.vector.tensor_scalar(out_three[:, part], y_three[:], inverse[:], None, mult)
         nc.sync.dma_start(out[0, :, 3 * P : DV], out_three[:])

from contextlib import ExitStack

import concourse.mybir as mybir
from concourse.masks import make_identity

F32 = mybir.dt.float32
BF16 = mybir.dt.bfloat16
U32 = mybir.dt.uint32
U16 = mybir.dt.uint16
U8 = mybir.dt.uint8
FP8X4 = mybir.dt.float8_e4m3fn_x4

P = 128
POOL = 2048
SLOTS = 512
NQ = 128
D = 512
DV = 512
PACK = 4
PAIRS = 2
PER_COLUMN = 16
PIECES = POOL // P
KB_FIRST = P - PIECES
QUARTERS = 2
VS_ROWS = slice(63, 128, 64)
HALF = SLOTS // 2
BANK = 2048
COLS = SLOTS // P
KIB = 1024

FLOPS = 2 * NQ * SLOTS * (D + DV)
BYTES = 4 * ((D + DV) * POOL + 2 * POOL + D * NQ + NQ * DV) + 2 * P * (SLOTS // PER_COLUMN)


def tile_attend_rbf_topk_kernel(tc, qT, kT, vT, vs, kb, offs, out):
    nc = tc.nc
    exp = mybir.ActivationFunctionType.Exp
    copy = mybir.ActivationFunctionType.Copy
    identity = mybir.ActivationFunctionType.Identity
    mult, subtract, minimum = mybir.AluOpType.mult, mybir.AluOpType.subtract, mybir.AluOpType.min

    with ExitStack() as ctx:
        keep = ctx.enter_context(tc.tile_pool(name="keep", bufs=1))
        over = ctx.enter_context(tc.tile_pool(name="over", bufs=1))
        psum = ctx.enter_context(tc.psum_pool(name="psum", bufs=1))

        def placed(name, shape, dtype, offset):
            return over.tile(shape, dtype, name=name, offset=offset, align_bytes=64)

        def bank(name, shape, number):
            return psum.tile(shape, F32, name=name, offset=number * BANK)

        def plane(window, t):
            return window[:, t * POOL : (t + 1) * POOL]

        def quantize(codes, scales, grouped):
            nc.vector.quantize_mx(out=codes.bitcast(FP8X4), scales=scales, in_=grouped)

        def product(y, lhs_codes, lhs_scales, codes, scales):
            nc.tensor.matmul_mx(
                out=y,
                lhsT=lhs_codes.bitcast(FP8X4),
                lhsT_scale=lhs_scales,
                rhs=codes.bitcast(FP8X4),
                rhs_scale=scales,
                start=True,
                stop=True,
            )

        offsets = keep.tile([P, SLOTS // PER_COLUMN], U16, name="offsets")
        halves = [slice(h * HALF, (h + 1) * HALF) for h in range(2)]

        def listed(slots):
            return offsets[:, slots.start // PER_COLUMN : slots.stop // PER_COLUMN]

        K_EARLY, K_TWO, K_THREE, V_ZERO, V_ONE, V_TWO, V_THREE = (KIB * at for at in (0, 16, 24, 32, 40, 48, 56))
        KB_ALL, NEG, Q_RAW, KB_WIN, VS_WIN = 64 * KIB, 66 * KIB, 68 * KIB, 72 * KIB, 80 * KIB
        k_rows = kT.rearrange("(m t) w -> m (t w)", t=PACK)
        k_early = placed("k_early", [P, 2 * POOL], F32, K_EARLY)
        k_late = [placed(f"k_late{t}", [P, POOL], F32, place) for t, place in enumerate((K_TWO, K_THREE))]
        v_zero = placed("v_zero", [P, POOL], F32, V_ZERO)
        v_one = placed("v_one", [P, POOL], F32, V_ONE)
        v_two = placed("v_two", [P, POOL], F32, V_TWO)
        v_three = placed("v_three", [P, POOL], F32, V_THREE)
        kb_rows = keep.tile([P, P], F32, name="kb_rows")
        vs_win = placed("vs_win", [P, POOL], F32, VS_WIN)
        q_raw = placed("q_raw", [P, PACK, NQ], F32, Q_RAW)
        nc.sync.dma_start(k_early[:], k_rows[:, 0 : 2 * POOL])
        nc.sync.dma_start(offsets[:], offs)
        nc.vector.memset(kb_rows[0:KB_FIRST, :], 0.0)
        nc.vector.memset(vs_win[0:63, 0 : POOL // 2], 0.0)
        nc.vector.memset(vs_win[64:P, 0 : POOL // 2], 0.0)
        nc.vector.memset(vs_win[0:127, POOL // 2 : POOL], 0.0)
        nc.scalar.dma_start(kb_rows[KB_FIRST:P, :], kb[0, :].rearrange("(r j) -> r j", j=P))
        for quarter, row in enumerate(range(P)[VS_ROWS]):
            tokens = slice(quarter * POOL // QUARTERS, (quarter + 1) * POOL // QUARTERS)
            nc.sync.dma_start(vs_win[row : row + 1, tokens], vs[0:1, tokens])
        for t in range(2):
            nc.sync.dma_start(k_late[t][:], k_rows[:, (2 + t) * POOL : (3 + t) * POOL])
        nc.sync.dma_start(q_raw[:], qT[0].rearrange("(m t) q -> m t q", t=PACK))
        nc.sync.dma_start(v_zero[:], vT[0:P, :])
        nc.sync.dma_start(v_one[:], vT[P : 2 * P, :])
        nc.sync.dma_start(v_two[:], vT[2 * P : 3 * P, :])
        nc.sync.dma_start(v_three[:], vT[3 * P : DV, :])

        ident = keep.tile([P, P], F32, name="ident")
        make_identity(nc, ident[:])

        kb_turn = bank("kb_turn", [P, P], 4)
        nc.tensor.transpose(kb_turn[:], kb_rows[:], ident[:])
        kb_col = keep.tile([P, PIECES], F32, name="kb_col")
        nc.scalar.copy(kb_col[:], kb_turn[:, KB_FIRST:P])
        kb_win = placed("kb_win", [P, POOL], F32, KB_WIN)
        for b in range(PIECES // COLS):
            spread = bank(f"kb_spread{b}", [P, COLS, P], (0, 1, 3, 5)[b])
            for c in range(COLS):
                r = b * COLS + c
                nc.tensor.transpose(spread[:, c, :], kb_col[:, r : r + 1].to_broadcast([P, P]), ident[:])
            nc.scalar.copy(kb_win[:, b * SLOTS : (b + 1) * SLOTS], spread[:].rearrange("p c j -> p (c j)"))
        kb_all = placed("kb_all", [P, SLOTS], F32, KB_ALL)
        nc.scalar.activation(kb_all[:], kb_win[:].indirect(offsets[:]), copy)
        vs_row = placed("vs_row", [P, SLOTS], F32, KB_WIN)
        nc.scalar.activation(vs_row[:], vs_win[:].indirect(offsets[:]), copy)
        vs_turn = bank("vs_turn", [P, PACK, P], 2)
        for t in range(PACK):
            nc.tensor.transpose(vs_turn[:, t, :], vs_row[:, t:SLOTS:PACK], ident[:])

        planes = keep.tile([P, 2, SLOTS], F32, name="planes")
        for t in range(2):
            nc.vector.tensor_copy(planes[:, t, :], plane(k_early, t).indirect(offsets[:]))
        k_grouped = placed("k_grouped", [P, SLOTS, PACK], BF16, K_EARLY)
        nc.vector.tensor_copy(k_grouped[:, :, 0:2], planes[:].rearrange("p t i -> p i t"))

        upper = placed("upper", [P, 2, HALF], F32, VS_WIN)
        for t in range(2):
            nc.vector.tensor_copy(k_grouped[:, halves[0], 2 + t], k_late[t][:].indirect(listed(halves[0])))
            nc.scalar.activation(upper[:, t, :], k_late[t][:].indirect(listed(halves[1])), copy)
        q_grouped = placed("q_grouped", [P, NQ, PACK], BF16, K_THREE)
        nc.scalar.copy(q_grouped[:], q_raw[:].rearrange("p t q -> p q t"))
        nc.vector.tensor_copy(k_grouped[:, halves[1], 2:4], upper[:].rearrange("p t i -> p i t"))

        k_codes = placed("k_codes", [P, SLOTS], U32, VS_WIN)
        k_scales = keep.tile([P, SLOTS], U8, name="k_scales", align_bytes=64)
        q_codes = keep.tile([P, NQ], U32, name="q_codes", align_bytes=64)
        q_scales = keep.tile([P, NQ], U8, name="q_scales", align_bytes=64)
        score = [bank(f"score{h}", [NQ, HALF], 3 + h) for h in range(2)]
        for h, half in enumerate(halves):
            quantize(k_codes[:, half], k_scales[:, half], k_grouped[:, half, :].rearrange("p i t -> p (i t)"))
            if h == 0:
                quantize(q_codes[:], q_scales[:], q_grouped[:].rearrange("p q t -> p (q t)"))
            product(score[h][:], q_codes[:], q_scales[:], k_codes[:, half], k_scales[:, half])

        g_zero = placed("g_zero", [P, SLOTS], BF16, Q_RAW)
        nc.scalar.activation(g_zero[:], v_zero[:].indirect(offsets[:]), copy)

        neg = placed("neg", [NQ, SLOTS], F32, NEG)
        for h, half in enumerate(halves):
            nc.vector.scalar_tensor_tensor(neg[:, half], score[h][:], -1.0, kb_all[:, half], mult, subtract)
        neg_m = keep.tile([NQ, 1], F32, name="neg_m")
        nc.vector.tensor_reduce(neg_m[:], neg[:], axis=mybir.AxisListType.X, op=minimum)
        vs_col = placed("vs_col", [P, PACK], F32, KB_ALL + KIB)
        nc.vector.tensor_reduce(vs_col[:], vs_turn[:, :, VS_ROWS], axis=mybir.AxisListType.X, op=mybir.AluOpType.add)

        p = placed("p", [NQ, PACK, P], F32, V_ZERO)
        sums = keep.tile([NQ, PAIRS], F32, name="sums")
        for u in range(PAIRS):
            nc.scalar.activation(
                p[:, 2 * u : 2 * u + 2, :].rearrange("q t m -> q m t"),
                neg[:].rearrange("q (m t) -> q m t", t=PACK)[:, :, 2 * u : 2 * u + 2],
                exp,
                bias=neg_m[:],
                scale=-1.0,
                accum_out=sums[:, u : u + 1],
            )
        p_turn = bank("p_turn", [P, PACK, NQ], 5)
        for t in range(PACK):
            nc.tensor.transpose(p_turn[:, t, :], p[:, t, :], ident[:])

        def turn(name, pair_words, number):
            turned = bank(name, [P, PAIRS, P], number)
            for u in range(PAIRS):
                nc.tensor.transpose(turned[:, u, :], pair_words(u), ident[:])
            return turned

        def in_order(gathered):
            words = gathered[:].bitcast(F32)
            return lambda u: words[:, u : SLOTS // 2 : PAIRS]

        def lay(grouped, turned, move):
            move(grouped.bitcast(F32).rearrange("p (e u) -> p e u", u=PAIRS), turned.rearrange("p u e -> p e u"))

        g_one = placed("g_one", [P, SLOTS], BF16, KB_ALL)
        nc.vector.tensor_copy(g_one[:], v_one[:].indirect(offsets[:]))
        total = keep.tile([NQ, 1], F32, name="total")
        nc.scalar.activation(total[:], sums[:, 0:1], identity, bias=sums[:, 1:2])
        turned_zero = turn("turned_zero", in_order(g_zero), 4)
        pair_grouped = placed("pair_grouped", [P, 2, P * PACK], BF16, NEG + 64)
        lay(pair_grouped[:, 0, :], turned_zero[:], nc.scalar.copy)
        turned_one = turn("turned_one", in_order(g_one), 4)

        w_grouped = keep.tile([P, NQ, PACK], BF16, name="w_grouped", align_bytes=64)
        nc.vector.tensor_tensor(
            w_grouped[:], p_turn[:].rearrange("p t q -> p q t"), vs_col[:].unsqueeze(1).to_broadcast([P, NQ, PACK]), mult
        )
        lay(pair_grouped[:, 1, :], turned_one[:], nc.vector.tensor_copy)
        w_codes = keep.tile([P, NQ], U32, name="w_codes", align_bytes=64)
        w_scales = keep.tile([P, NQ], U8, name="w_scales", align_bytes=64)
        quantize(w_codes[:], w_scales[:], w_grouped[:].rearrange("p q t -> p (q t)"))
        inverse = placed("inverse", [NQ, 1], F32, V_ONE)
        nc.vector.reciprocal(inverse[:], total[:])
        pair_codes = keep.tile([P, 2 * P], U32, name="pair_codes", align_bytes=64)
        pair_scales = keep.tile([P, 2 * P], U8, name="pair_scales", align_bytes=64)
        quantize(pair_codes[:], pair_scales[:], pair_grouped[:].rearrange("p b x -> p (b x)"))
        y_pair = bank("y_pair", [NQ, 2 * P], 6)
        product(y_pair[:], w_codes[:], w_scales[:], pair_codes[:], pair_scales[:])

        g_two = placed("g_two", [P, SLOTS], BF16, V_ONE + KIB)
        nc.scalar.activation(g_two[:], v_two[:].indirect(offsets[:]), copy)
        turned_two = turn("turned_two", in_order(g_two), 1)

        g_three = placed("g_three", [P, SLOTS], BF16, NEG + KIB)
        nc.vector.tensor_copy(g_three[:, halves[0]], v_three[:].indirect(listed(halves[0])))
        nc.scalar.activation(g_three[:, halves[1]], v_three[:].indirect(listed(halves[1])), copy)
        turned_three = turn("turned_three", in_order(g_three), 3)

        two_grouped = placed("two_grouped", [P, P * PACK], BF16, V_THREE)
        lay(two_grouped[:], turned_two[:], nc.scalar.copy)
        out_pair = placed("out_pair", [NQ, 2 * P], F32, V_THREE + KIB)
        nc.vector.tensor_scalar(out_pair[:], y_pair[:], inverse[:], None, mult)
        nc.sync.dma_start(out[0, :, 0 : 2 * P], out_pair[:])

        two_codes = keep.tile([P, P], U32, name="two_codes", align_bytes=64)
        two_scales = keep.tile([P, P], U8, name="two_scales", align_bytes=64)
        quantize(two_codes[:], two_scales[:], two_grouped[:])
        three_grouped = keep.tile([P, P * PACK], BF16, name="three_grouped", align_bytes=64)
        three_codes = keep.tile([P, P], U32, name="three_codes", align_bytes=64)
        three_scales = keep.tile([P, P], U8, name="three_scales", align_bytes=64)
        parts = [slice(j * P // 2, (j + 1) * P // 2) for j in range(2)]
        for part in parts:
            wide = slice(part.start * PACK, part.stop * PACK)
            lay(three_grouped[:, wide], turned_three[:, :, part], nc.scalar.copy)
            quantize(three_codes[:, part], three_scales[:, part], three_grouped[:, wide])

        y_two = bank("y_two", [NQ, P], 5)
        product(y_two[:], w_codes[:], w_scales[:], two_codes[:], two_scales[:])
        out_two = keep.tile([NQ, P], F32, name="out_two")
        nc.scalar.activation(out_two[:], y_two[:], copy, scale=inverse[:])
        nc.sync.dma_start(out[0, :, 2 * P : 3 * P], out_two[:])

        out_three = keep.tile([NQ, P], F32, name="out_three")
        for j, part in enumerate(parts):
            y_three = bank(f"y_three{j}", [NQ, P // 2], (7, 4)[j])
            product(y_three[:], w_codes[:], w_scales[:], three_codes[:, part], three_scales[:, part])
            nc.vector.tensor_scalar(out_three[:, part], y_three[:], inverse[:], None, mult)
        nc.sync.dma_start(out[0, :, 3 * P : DV], out_three[:])
